import numpy as np, ml_dtypes
CORES = [1,5,17,21,33,37,49,53]
N = 8
import mx_ref
BF = ml_dtypes.bfloat16
def gentries(a):
    return np.ascontiguousarray(a.reshape(8, 16, -1).transpose(0, 2, 1)).reshape(8, -1)
def gtable(e):
    e = np.asarray(e); return np.ascontiguousarray(e.reshape(8, -1, 16).transpose(0, 2, 1)).reshape(128, -1).astype(np.int32)
def gcols(t, e):
    v = np.concatenate([t.reshape(8, 16, -1, 4), np.zeros((8, 16, 1, 4), BF)], axis=2)
    return np.ascontiguousarray(np.stack([v[g][:, e[g]] for g in range(8)])).reshape(128, -1)
def tile(rs):
    return np.stack(rs, axis=2).reshape(128, -1).astype(BF)
def pick(q, e):
    c = np.concatenate([q[0].reshape(128, -1, 4), np.zeros((128, 1, 4), np.uint8)], axis=1); s = np.concatenate([q[1], np.ones((16, 1), np.uint8)], axis=1)
    return (np.ascontiguousarray(c[:, e].reshape(128, -1)), np.ascontiguousarray(s[:, e]))
def join(*qs):
    return (np.concatenate([q[0] for q in qs], axis=1), np.concatenate([q[1] for q in qs], axis=1))
def put(q, e, v):
    c, s = q[0].reshape(128, -1, 4).copy(), q[1].copy(); c[:, e] = v[0].reshape(128, -1, 4); s[:, e] = v[1]
    return (c.reshape(128, -1), s)
def pk(c, s):
    return (np.ascontiguousarray(c), mx_ref.live(s))
def emit(q):
    return q[0], q[1]
def packed(v, rng):
    q = [mx_ref.quantize(np.ascontiguousarray(v[r])) for r in range(N)]
    return np.stack([a for a, b in q]), np.stack([mx_ref.plane(b, rng) for a, b in q])
def values_of_codes():
    e, c = np.zeros((128, 128, 4), np.float32), np.zeros((128, 2, 4), np.uint8)
    e[np.arange(128), np.arange(128), 0] = 1
    c[:127, :, 0] = np.arange(256).reshape(2, 128).T[:127]
    return mx_ref.matmul(mx_ref.quantize(e.reshape(128, 512).astype(BF)), (c.reshape(128, 8), np.full((16, 2), 127, np.uint8))).T.reshape(-1).astype(np.float64)
CODE_VALUE, SCALE_VALUE = values_of_codes(), 2.0 ** (np.arange(256) - 127.0)
def decode(q):
    return (CODE_VALUE[q[0]].reshape(16, 8, -1, 4) * SCALE_VALUE[q[1]][:, None, :, None] + 0.0).reshape(128, -1).astype(np.float32)
def f(rng, *shape):
    return mx_ref.flush((rng.standard_normal(shape, dtype=np.float32) * np.exp2(rng.integers(-2, 3, shape[:-1] + (1,)))).astype(BF))
def wide(rng, *shape, cols=0):
    v = rng.standard_normal(shape, dtype=np.float32) * np.exp2(rng.integers(-12, 13, shape)).astype(np.float32)
    if cols: v *= np.repeat(np.exp2(rng.integers(-cols, cols + 1, shape[:-2] + (1, shape[-1] // 4))) * (rng.random(shape[:-2] + (1, shape[-1] // 4)) > 0.0625), 4, axis=-1).astype(np.float32)
    return mx_ref.flush(v.astype(BF))
C, J = 256, 128
STEP = [1, 2, 4]
def big(v):
    v = v.astype(np.float32)
    v[np.abs(v) < np.float32(2.0 ** -12)] = 0
    return v.astype(BF)
def numbers_of(rng):
    return {"x": big(f(rng, N, 128, 4 * C)), "u": np.array(f(rng, N, 128, 512)), "v": np.array(f(rng, N, 128, 512))}
def maps_of(rng):
    return rng.permuted(np.tile(np.arange(C), (N, 8, 1)), axis=2)
def arrivals(rng, m, right=0.75):
    return np.where(rng.random((N, 8, 4, C)) < right, m[:, :, None], rng.integers(0, C, (N, 8, 4, C)))
def lists(m, a):
    return {"mp": np.stack([gtable(m[r]) for r in range(N)]), "ar": np.stack([gtable(a[r].reshape(8, 4 * C)) for r in range(N)])}
def layers(rng):
    return big(f(rng, N, 128, 2048)).reshape(N, 128, 4, 128, 4)
def weights(rng, w):
    c, s = packed(np.ascontiguousarray(w).reshape(N, 128, 2048), rng)
    return {"wc": c, "ws": s}
def setup_inputs(rng):
    m = maps_of(rng)
    return {**numbers_of(rng), **lists(m, arrivals(rng, m)), **weights(rng, layers(rng))}
def setup_inputs_ties(rng):
    d = numbers_of(rng)
    o = rng.permutation(N)
    x = d["x"].reshape(N, 128, C, 4)
    x[:, :8, :, :2] = rng.integers(0, 3, (N, 8, C, 2)).astype(np.float32).astype(BF)
    x[:, 8:16, :, :2] = 1
    x[o[0], :16, :, :2] = 0
    u = d["u"].reshape(N, 128, 128, 4)
    u[:, :, ::16] = 0
    u[:, :, 1::16] = 0
    w = layers(rng)
    for e in range(2):
        for p in range(16):
            w[:, :, e, p] = 0
            w[:, p, e, p, e] = 32
        for g in range(8):
            for h in range(0, 16, 8):
                w[:, :, e, 16 * g + h] = 0
                w[:, g + h, e, 16 * g + h, e] = 32
                u[:, 16 * g + h, 16 * g + e, e] = 1.0 if h == 0 else -1.0
    m = maps_of(rng)
    for r in range(N): m[r, 1:] = rng.permutation(C)[:8][rng.integers(0, 8, (7, C))]
    one = int(o[1])
    goal = int(m[one, 1, 0])
    m[one, 1] = goal
    right = np.array([1.0, 0.75] + [0.25] * 6)[:, None, None]
    a = arrivals(rng, m, right)
    a[one, 1] = m[one, 1]
    a[one, 2, :, goal] = (m[one, 2, goal] + 1 + np.arange(4)) % C
    x[one, 2, m[one, 0, :J], :2] = 0
    x[one, 2, m[one, 0, 0], :2] = 2
    return {"x": x.reshape(N, 128, 4 * C), "u": u.reshape(N, 128, 512), "v": d["v"], **lists(m, a), **weights(rng, w)}
def setup_inputs_near(rng):
    d = numbers_of(rng)
    x = d["x"].reshape(N, 128, C, 4)
    x.reshape(N, 8, 16, C, 4)[:, :, 8:] = 1
    u = d["u"].reshape(N, 128, 128, 4)
    u[:, :, ::16] = 0
    u[:, :, 1::16] = 0
    o = rng.permutation(N) % 4
    m = maps_of(rng)
    for r in range(N):
        t = np.array([[9.0, 8.0], [11.0, 10.0], [10.0, 9.0]])[rng.integers(0, 3, (8, C, 2))].reshape(8, C, 4) * 0.125
        far = m[r, 0, rng.permutation(J)[:12]]
        if o[r] % 2 == 0: t = t * 2.0 ** -12
        if o[r] < 2:
            t[:, far[:8]] *= 2.0 ** 25 if o[r] == 0 else 2.0 ** 13
            x[r, 15] = 0
            x[r, 15, far[8:], 0] = 1
        x[r, :8] = t.astype(np.float32).astype(BF)
        k = 2.0 ** -30 if o[r] % 2 == 0 else 1.0
        for h in range(0, 128, 16):
            for b in range(2):
                u[r, h + 8 + 2 * b, h + b, 0] = 1.125 * k
                u[r, h + 9 + 2 * b, h + b, 0] = -1.25 * k
                if o[r] < 2: u[r, 16, h + b, 0] = 2.0 ** 30
    w = layers(rng)
    w.reshape(N, 128, 4, 8, 16, 4)[:, :, :, :, 8:] = 0
    w[:, :, :, :8] = 0
    w[:, :, 0, 16] = 0
    w[:, 15, 0, 16, 0] = 32
    for g in range(8):
        for i in range(4):
            w[:, g, i, g, i] = 32
            w[:, g, 0, 16 * g + 8 + i, i] = 2.0 ** -13
    return {"x": x.reshape(N, 128, 4 * C), "u": u.reshape(N, 128, 512), "v": d["v"], **lists(m, arrivals(rng, m)), **weights(rng, w)}
def setup_inputs_ends(rng):
    o = rng.permutation(N) % 4
    x = rng.choice([-1.0, 1.0], (N, 128, 4 * C))
    u = rng.choice([-1.0, 1.0], (N, 128, 128, 4))
    v = rng.choice([-1.0, 1.0], (N, 128, 512))
    m, a = np.zeros((N, 8, C), int), np.full((N, 8, 4, C), C - 1)
    for r in range(N):
        if o[r] == 0:
            x[r] = 1.0
            u[r] = u[r, :1, :, :1].copy()
        if o[r] % 2 == 0: m[r] = C - 1
        if o[r] == 2: a[r, :, ::3] = 0
        if o[r] == 3:
            x[r] = -1.0
            m[r] = np.arange(C)
            a[r] = np.arange(C)[::-1]
        x[r] *= 2.0 ** -12 if o[r] == 2 else 2.0 ** 14
        u[r] *= 2.0 ** -30 if o[r] == 2 else 2.0 ** 30
        v[r] *= 2.0 ** -30 if o[r] == 2 else 2.0 ** 30
    w = np.full((N, 128, 4, 128, 4), 4.0)
    w[:, :, :3, :, :2] = 8.0
    w[:, :, :3, :, 2:] = 0.0
    w[:, :, 3] *= rng.choice([-1.0, 1.0], (N, 128, 128, 4))
    return {"x": x.astype(BF), "u": u.reshape(N, 128, 512).astype(BF), "v": v.astype(BF), **lists(m, a), **weights(rng, w.astype(BF))}
def setup_inputs_blocks(rng):
    d = numbers_of(rng)
    s = (1.0 + (2 * rng.integers(0, 64, (N, 16, 8, C, 4)) + 1) * 2.0 ** -7) * np.exp2(-rng.integers(8, 15, (N, 16, 8, C, 4)).astype(np.float64))
    top = np.arange(32).reshape(8, 1, 4) == rng.integers(0, 32, (N, 16, C))[:, :, None, :, None]
    x = np.where(top, 1.96875, s) * rng.choice([-1.0, 1.0], (N, 16, 8, C, 4)) * np.exp2(rng.integers(2, 8, (N, 16, 1, C, 1)).astype(np.float64))
    m = maps_of(rng)
    return {"x": x.reshape(N, 128, 4 * C).astype(np.float32).astype(BF), "u": d["u"], "v": d["v"], **lists(m, arrivals(rng, m)), **weights(rng, layers(rng))}
def setup_inputs_spread(rng):
    d = setup_inputs(rng)
    d["x"] = big(wide(rng, N, 128, 4 * C, cols=4).astype(np.float32) * np.float32(2.0 ** -5))
    return d
def check_inputs(d):
    b = []
    for k, lo, hi in (("x", 2.0 ** -12, 2.0 ** 14), ("u", 2.0 ** -30, 2.0 ** 30), ("v", 2.0 ** -30, 2.0 ** 30)):
        a = np.abs(d[k].astype(np.float32))
        if not (np.isfinite(a).all() and ((a == 0) | (a >= lo) & (a <= hi)).all()): b.append("a value of " + k)
    for k in ("mp", "ar"):
        if not ((d[k] >= 0) & (d[k] < C)).all(): b.append("an entry of " + k)
    none, least, most = [emit(mx_ref.quantize(np.full((128, 16), k, np.float32).astype(BF)))[1][0, 0] for k in (0.0, 2.0 ** -30, 2.0 ** 30)]
    for r in range(N):
        if ((d["wc"][r] == 0x7F) | (d["wc"][r] == 0xFF)).any(): b.append("wc: a code that is no number")
        s = mx_ref.live(d["ws"][r])
        if ((s != none) & ((s < least) | (s > most))).any(): b.append("ws: a scale out of range")
        else:
            a = np.abs(decode(pk(d["wc"][r], d["ws"][r]))).reshape(128, 512, 4)
            if (np.sum(a, axis=(0, 2), dtype=np.float64) > 2048).any(): b.append("a column of W")
    return b
def chains(m):
    e = [np.arange(J)]
    for g in range(8): e.append(m[g, e[g]])
    return np.stack(e[:8]), np.stack(e[1:])
def reference(x, u, v, mp, ar, wc, ws):
    qu = [mx_ref.quantize(u[r]) for r in range(N)]
    lay = [pk(wc[r], ws[r]) for r in range(N)]
    now = [x[r] for r in range(N)]
    maps = np.stack([gentries(mp[r]) for r in range(N)])
    cand = np.stack([gentries(ar[r]).reshape(8, 4, C) for r in range(N)])
    grp = np.arange(8)
    for h in STEP:
        for r in range(N):
            donor = (r + h) % N
            old = decode(mx_ref.quantize(now[r])).astype(BF)
            e, l = chains(maps[r])
            m = mx_ref.quantize(gcols(old, l))
            q = mx_ref.quantize(tile([np.maximum(mx_ref.matmul(pick(lay[donor], np.arange(128 * b, 128 * b + 128)), m), np.float32(0.0)) * np.float32(0.03125) for b in range(4)]))
            s = mx_ref.matmul(qu[r], q)
            a = cand[r][grp[:, None], 2 * (s[::16] > 0) + (s[1::16] > 0), e]
            wrong = a != l
            first = np.argmax(wrong, axis=0)
            for j in range(J - 1, -1, -1):
                g = first[j]
                if wrong[g, j]: maps[r, g, e[g, j]] = a[g, j]
            l = chains(maps[r])[1]
            n = np.tile(J + np.arange(C), (8, 1))
            for j in range(J - 1, -1, -1): n[grp, l[:, j]] = j
            other = gcols(np.concatenate([decode(q).astype(BF), old], axis=1), n)
            now[r] = ((old.astype(np.float32) + other.astype(np.float32)) * np.float32(0.5)).astype(BF)
    y, fo = np.zeros((N, 128, C), np.float32), np.zeros((N, 8, C), np.float32)
    oc, osc = np.zeros((N, 128, 4 * C), np.uint8), np.zeros((N, 16, C), np.uint8)
    for r in range(N):
        q = mx_ref.quantize(now[r])
        y[r] = mx_ref.matmul(mx_ref.quantize(v[r]), q)
        fo[r] = maps[r]
        oc[r], osc[r] = emit(q)
    return {"y": y, "fo": fo, "oc": oc, "osc": osc}

@@ -1,0 +1,506 @@
+from concourse.bass import DstId, RemoteDMATransfer
+from concourse.mybir import dt, AluOpType as A, AxisListType, ActivationFunctionType as F
+
+N = 8
+STEP = [1, 2, 4]
+UNIT = 512.0
+P21 = 2097152.0
+ROUND = 12582912.0
+SCRATCH = {}
+SEMAPHORES = ["cv", "cs", "ct", "cg", "am0", "am1", "ah0", "ah1", "aw"] + ["d%d" % i for i in range(24)] + ["l%d" % i for i in range(16)]
+
+
+def _sb(name, n, dtype="float32"):
+    SCRATCH[name] = ("sbuf", [128, n], dtype)
+
+
+def _mx(name, n):
+    _sb(name, n, "float8_e4m3fn_x4")
+    _sb(name + "_s", n, "uint8")
+
+
+for _b in range(4):
+    SCRATCH["pa%d" % _b] = ("psum", [128, 512], "float32")
+    SCRATCH["pb%d" % _b] = ("psum", [128, 512], "float32")
+    _sb("win%d" % _b, 384, "bfloat16")
+    _mx("qx%d" % _b, 384)
+for _n, _k in [("qe", 512), ("qm", 384), ("qml", 256), ("qh", 256), ("qw", 512), ("qwl", 512), ("qu", 128), ("qup", 128), ("qv", 128)]:
+    _mx(_n, _k)
+for _n, _k in [("oth", 512), ("fh", 512), ("xt", 1024), ("ut", 512), ("vt", 512), ("mt", 512), ("ht", 512), ("nx", 1024), ("zt", 528), ("zs", 528),
+               ("cini", 512), ("itz", 272), ("sl", 128), ("inv", 544), ("t512", 512)]:
+    _sb(_n, _k, "bfloat16")
+for _n, _k in [("offa", 128), ("aro", 64), ("off", 18), ("offm", 8), ("offe", 8), ("offr", 8), ("oo", 8), ("ul", 8), ("offi", 16), ("noff", 16), ("cil", 32)]:
+    _sb(_n, _k, "uint16")
+for _n, _k in [("mpa", 128), ("ari", 64), ("ci8", 8), ("fi", 8)]:
+    _sb(_n, _k, "int32")
+for _n, _k in [("ra", 1024), ("it", 256), ("map", 2304), ("cw", 256), ("cwa", 256), ("cf", 32), ("tlx", 288), ("gc", 144), ("grow", 64), ("rt", 128), ("tt", 128),
+               ("rte", 128), ("tte", 128), ("cr", 128), ("ctr", 128), ("c32", 32), ("e8", 8), ("k1", 32), ("eq", 32), ("key", 32), ("g32", 32), ("kab", 64),
+               ("sig", 64), ("gi", 32), ("fl", 64), ("wp", 64), ("u1", 32), ("uu", 40), ("rr", 8), ("cu", 32), ("x64", 64), ("d32", 32), ("t1", 32), ("e32", 32),
+               ("m32", 32), ("l32", 32), ("t64", 64), ("p64", 64), ("row", 256), ("t2", 256), ("oof", 16), ("ulf", 8), ("tri", 32), ("i32", 32), ("kk", 128),
+               ("ki", 128), ("v32", 32), ("h32", 32), ("gc0", 16), ("brow", 128), ("e128", 128), ("sc", 128), ("p1", 8), ("p2", 8), ("p3", 8), ("n16", 16),
+               ("yt", 256)]:
+    _sb(_n, _k)
+
+CODES = {n for n, s in SCRATCH.items() if s[2] == "float8_e4m3fn_x4"}
+PSUM = {n for n, s in SCRATCH.items() if s[0] == "psum"}
+
+
+def rank_program(g, core, T, topo):
+    rank = T.rank_of(core)
+    if rank is None:
+        return
+    Q = {"g": g, "v": g.vector, "s": g.scalar, "t": g.tensor, "y": g.sync}
+    known = {q: {} for q in Q}
+    hist = {}
+    count = {}
+    nd = [1]
+    nl = [0]
+
+    def w(name, c0=0, c1=None, p0=0, p1=128, st=1):
+        t = T[name]
+        if c1 is None:
+            c1 = t.shape[1]
+        if p0 == 0 and p1 == 128:
+            ap = t[:, c0:c1] if st == 1 else t[:, c0:c1:st]
+        else:
+            ap = t[p0:p1, c0:c1] if st == 1 else t[p0:p1, c0:c1:st]
+        return (ap, name, p0, p1, c0, c1, st)
+
+    def overlap(a, b):
+        if a[2] >= b[3] or b[2] >= a[3] or a[4] >= b[5] or b[4] >= a[5]:
+            return False
+        return not (a[6] == b[6] and a[6] > 1 and (a[4] - b[4]) % a[6])
+
+    def covers(a, b):
+        return a[2] <= b[2] and a[3] >= b[3] and a[4] <= b[4] and a[5] >= b[5] and (a[6] == 1 or (a[6] == b[6] and (a[4] - b[4]) % a[6] == 0))
+
+    def order(q, reads, writes, compute):
+        need = []
+        for isw, vs in ((False, reads), (True, writes)):
+            for x in vs:
+                for (y, yw, yq, sem, val, clock, ycomp) in hist.get(x[1], []):
+                    same = yq == q and compute and ycomp
+                    if same and not yw:
+                        continue
+                    if x[1] not in PSUM and (not overlap(x, y) or not (isw or yw)):
+                        continue
+                    need.append((sem, val, clock))
+        for sem, val, clock in reversed(need):
+            if known[q].get(sem, 0) >= val:
+                continue
+            Q[q].wait_ge(T.sem[sem], val)
+            for k, n in clock.items():
+                if known[q].get(k, 0) < n:
+                    known[q][k] = n
+            known[q][sem] = val
+
+    def note(q, reads, writes, sem, val, compute):
+        clock = dict(known.get(q, {}))
+        for isw, vs in ((False, reads), (True, writes)):
+            for x in vs:
+                h = hist.setdefault(x[1], [])
+                if isw:
+                    h[:] = [r for r in h if not covers(x, r[0])]
+                h.append((x, isw, q, sem, val, clock, compute))
+
+    def op(q, call, writes, reads):
+        order(q, reads, writes, True)
+        sem = "c" + q
+        count[sem] = count.get(sem, 0) + 1
+        call().then_inc(T.sem[sem], 1)
+        note(q, reads, writes, sem, count[sem], True)
+
+    def dma(q, out, in_, reads=(), writes=(), group=None):
+        order(q, reads, writes, False)
+        if group is None:
+            sem = "d%d" % nd[0]
+            nd[0] += 1
+            total = 16
+        else:
+            sem, total = group
+        count[sem] = total
+        Q[q].dma_start(out, in_).then_inc(T.sem[sem], 16)
+        note(q, reads, writes, sem, total, False)
+
+    def raw(x):
+        return x[0].bitcast(dt.uint8) if x[1] in CODES else x[0]
+
+    def send(to, src, dst, sem):
+        dc = T.cores[to]
+        order("g", [src], [], False)
+        rid, pid, _ = topo.addr(dc)
+        l = "l%d" % nl[0]
+        nl[0] += 1
+        g.remote_dma(raw(dst), raw(src), T.sem[sem], T.sem[l], pid, rid, topo.mask(core, dc))
+        count[l] = len(topo.engines(core, dc))
+        note("g", [src], [], l, count[l], False)
+
+    def expect(frm, views, sem):
+        n = len(topo.engines(T.cores[frm], core)) * len(views)
+        count[sem] = n
+        note("x", [], views, sem, n, False)
+
+    def copy(out, in_, q="v"):
+        if q == "v":
+            op("v", lambda: g.vector.tensor_copy(out[0], in_[0]), [out], [in_])
+        else:
+            op("s", lambda: g.scalar.activation(out[0], in_[0], F.Copy), [out], [in_])
+
+    def pick(out, win, off, q="v", scale=None):
+        rd = [win, off]
+        if q == "v":
+            if scale is None:
+                op("v", lambda: g.vector.tensor_copy(out[0], win[0].indirect(off[0])), [out], rd)
+            else:
+                op("v", lambda: g.vector.tensor_scalar(out[0], win[0].indirect(off[0]), scale, None, A.mult), [out], rd)
+        elif scale is None:
+            op("s", lambda: g.scalar.activation(out[0], win[0].indirect(off[0]), F.Copy), [out], rd)
+        elif isinstance(scale, float):
+            op("s", lambda: g.scalar.activation(out[0], win[0].indirect(off[0]), F.Copy, scale=scale), [out], rd)
+        else:
+            op("s", lambda: g.scalar.activation(out[0], win[0].indirect(off[0]), F.Copy, scale=scale[0]), [out], rd + [scale])
+
+    def scatter(win, off, in_):
+        op("v", lambda: g.vector.tensor_copy(win[0].indirect(off[0]), in_[0]), [win], [off, in_])
+
+    def tt(out, a, b, o):
+        op("v", lambda: g.vector.tensor_tensor(out[0], a[0], b[0], o), [out], [a, b])
+
+    def ts(out, a, s1, s2, o1, o2=None):
+        rd = [a] + [s for s in (s1, s2) if isinstance(s, tuple)]
+        x1 = s1[0] if isinstance(s1, tuple) else s1
+        x2 = s2[0] if isinstance(s2, tuple) else s2
+        if o2 is None:
+            op("v", lambda: g.vector.tensor_scalar(out[0], a[0], x1, None, o1), [out], rd)
+        else:
+            op("v", lambda: g.vector.tensor_scalar(out[0], a[0], x1, x2, o1, o2), [out], rd)
+
+    def scan(out, d0, d1):
+        op("v", lambda: g.vector.tensor_tensor_scan(out[0], d0[0], d1[0], 0.0, A.max, A.mult), [out], [d0, d1])
+
+    def turn(out, a):
+        op("v", lambda: g.vector.transpose(out[0], a[0]), [out], [a])
+
+    def fill(out, c):
+        op("v", lambda: g.vector.memset(out[0], c), [out], [])
+
+    def iota(out, pattern, base, cm):
+        op("g", lambda: g.iota(out[0], pattern, base, cm, allow_small_or_imprecise_dtypes=True), [out], [])
+
+    def quant(name, tile, c0=0, n=128, t0=0):
+        o, s, i = w(name, c0, c0 + n), w(name + "_s", c0, c0 + n), w(tile, t0, t0 + 4 * n)
+        op("v", lambda: g.vector.quantize_mx(o[0], s[0], i[0]), [o, s], [i])
+
+    def mm(ps, n, l, lc, r, rc=0):
+        o = w(ps, 0, n)
+        a, b, c, d = w(l, lc, lc + 128), w(l + "_s", lc, lc + 128), w(r, rc, rc + n), w(r + "_s", rc, rc + n)
+        op("t", lambda: g.tensor.matmul_mx(o[0], a[0], b[0], c[0], d[0], True, True), [o], [a, b, c, d])
+
+    for q, h in (("y", 0), ("s", 1)):
+        for m in range(8):
+            dma(q, T.mpa[16 * h:16 * h + 16, 16 * m:16 * m + 16], T.mp[16 * m:16 * m + 16, :], (), [w("mpa", 16 * m, 16 * m + 16, 16 * h, 16 * h + 16)], ("d0", 256))
+        if h == 0:
+            dma("y", T.xt[:], T.x[:], (), [w("xt")])
+    dma("s", T.ari[:], T.ar[:], (), [w("ari")])
+    dma("y", T.qw[:].bitcast(dt.uint8), T.wc[:], (), [w("qw")])
+    dma("y", T.qw_s[:], T.ws[:], (), [w("qw_s")])
+    dma("s", T.ut[:], T.u[:], (), [w("ut")])
+    dma("s", T.vt[:], T.v[:], (), [w("vt")])
+
+    iota(w("ci8", 0, 1), [[1, 1]], 0, 1)
+    iota(w("gc0"), [[-1, 16]], 127, -1)
+    iota(w("it"), [[1, 256]], 0, 0)
+    iota(w("i32"), [[1, 32]], 0, 0)
+    iota(w("kab", 0, 32), [[0, 8], [1, 2], [0, 2]], 0, 0)
+    iota(w("kab", 32, 64), [[0, 16], [1, 2]], 0, 0)
+    fill(w("zs"), 0.5)
+    fill(w("cu"), 1.0 / UNIT)
+    z = w("zt", 0, 516)
+    zs = w("zs", 0, 516)
+    op("g", lambda: g.affine_select(z[0], zs[0], [[-1, 516]], A.is_equal, 0.0, 3, 4), [z], [zs])
+    iota(w("gi"), [[1, 8], [0, 4]], 0, 0)
+    iota(w("ki"), [[0, 8], [1, 16]], 0, 0)
+    iota(w("v32"), [[16, 16], [0, 2]], -256, 0)
+    iota(w("h32"), [[0, 16], [1, 2]], 0, 0)
+    iota(w("sl"), [[1, 128]], 0, 0)
+    iota(w("itz", 0, 256), [[1, 256]], -256, 0)
+
+    def bits(c, sh, m):
+        o, i = w("ci8", c, c + 1), w("ci8", 0, 1)
+        if sh:
+            op("v", lambda: g.vector.tensor_scalar(o[0], i[0], sh, m, A.arith_shift_right, A.bitwise_and), [o], [i])
+        else:
+            op("v", lambda: g.vector.tensor_scalar(o[0], i[0], m, None, A.bitwise_and), [o], [i])
+    bits(1, 0, 15)
+    bits(2, 4, 1)
+    bits(3, 0, 31)
+    bits(4, 2, 3)
+    copy(w("cf", 0, 5), w("ci8", 0, 5))
+
+    def cf(c):
+        return w("cf", c, c + 1)
+    PP, QQ, HH, II, KR, H16, TQ, TJ, TJC = [cf(c) for c in range(9)]
+    MK = [cf(12 + k) for k in range(4)]
+    ts(w("tlx", 0, 1), PP, -1.0, 127.0, A.mult, A.add)
+    ts(cf(10), HH, 32.0, -16.0, A.mult, A.add)
+    tt(w("tlx", 16, 17), w("tlx", 0, 1), cf(10), A.add)
+    copy(w("off", 0, 2), w("tlx", 0, 32, st=16))
+    ts(H16, HH, 16.0, None, A.mult)
+    ts(w("gc", 0, 16), w("gc0"), QQ, None, A.add)
+    ts(TQ, QQ, 512.0, None, A.add)
+    ts(TJ, PP, 2048.0, None, A.add)
+    ts(TJC, TJ, ROUND, None, A.add)
+    ts(w("uu", 32, 33), TJ, UNIT, None, A.mult)
+    for k in range(4):
+        ts(MK[k], KR, float(k), None, A.is_equal)
+    ts(w("oof", 0, 1), QQ, H16, None, A.add)
+    ts(cf(11), QQ, 16.0, None, A.add)
+    tt(w("oof", 1, 2), cf(11), H16, A.subtract)
+    ts(w("oof", 2, 4), w("oof", 0, 2), 32.0, None, A.add)
+    copy(w("oo", 0, 4), w("oof", 0, 4))
+    fill(w("ulf"), 0.0)
+    ts(w("ulf", 0, 1), KR, 16.0, None, A.mult)
+    ts(w("ulf", 1, 2), KR, 16.0, 64.0, A.mult, A.add)
+    ts(w("ulf", 2, 4), w("ulf", 0, 2), 1.0, None, A.add)
+    copy(w("ul"), w("ulf"))
+
+    def late_constants():
+        ts(w("tri"), w("i32"), II, None, A.is_gt)
+        ts(w("sig"), w("kab"), -2.0 * P21, P21, A.mult, A.add)
+        tt(w("g32"), w("kab", 0, 32), w("kab", 32, 64), A.add)
+        ts(w("g32"), w("g32"), P21, None, A.mult)
+        ts(w("gi"), w("gi"), 256.0 * UNIT, None, A.mult)
+        tt(w("g32"), w("g32"), w("gi"), A.add)
+        ts(w("kk"), w("ki"), QQ, None, A.is_gt)
+        ts(w("kk", 15, 128, st=16), w("kk", 15, 128, st=16), TQ, None, A.mult)
+        ts(w("h32"), w("h32"), HH, None, A.is_equal)
+        ts(w("v32"), w("v32"), QQ, None, A.add)
+        tt(w("v32"), w("v32"), w("h32"), A.mult)
+        ts(w("cil"), w("v32"), 256.0, None, A.add)
+        fill(w("itz", 256, 272), -256.0)
+        pick(w("cini"), w("itz"), w("cil"), "s")
+        quant("qu", "ut")
+        quant("qv", "vt")
+        o, i, l = w("qup"), w("qu"), w("ul")
+        op("v", lambda: g.vector.tensor_copy(o[0].bitcast(dt.uint32), i[0].bitcast(dt.uint32).indirect(l[0])), [o], [i, l])
+        o2, i2 = w("qup_s"), w("qu_s")
+        op("v", lambda: g.vector.tensor_copy(o2[0], i2[0].indirect(l[0])), [o2], [i2, l])
+
+    def candidates():
+        copy(w("aro"), w("ari"))
+        for k in range(4):
+            pick(w("ra", 256 * k, 256 * k + 256), w("it"), w("aro", 16 * k, 16 * k + 16), "s", MK[k])
+        tt(w("cw"), w("ra", 0, 256), w("ra", 256, 512), A.add)
+        tt(w("cwa"), w("ra", 512, 768), w("ra", 768, 1024), A.add)
+        tt(w("cw"), w("cw"), w("cwa"), A.add)
+
+    for a in range(4):
+        copy(w("offa", 0, 128, 32 * a, 32 * a + 32), w("mpa", 0, 128, 0, 32))
+
+    def mapw(m):
+        return w("map", 256 * m, 256 * m + 256)
+    for m in range(8):
+        if m not in (3, 6):
+            pick(mapw(m), w("it"), w("offa", 16 * m, 16 * m + 16), "v" if m == 0 else "s")
+
+    def hop(m):
+        gr = w("grow", 32 * (m % 2), 32 * (m % 2) + 32)
+        gc = w("gc", 16 * m + 16, 16 * m + 32)
+        t = 32 * m + 32
+        if m == 7:
+            pick(gc, mapw(m), w("off", 2 * m, 2 * m + 1))
+            return
+        pick(gr, mapw(m), w("off", 2 * m, 2 * m + 2))
+        pick(gc, mapw(m), w("off", 2 * m, 2 * m + 1), "s")
+        turn(w("tlx", t, t + 32), gr)
+        copy(w("off", 2 * m + 2, 2 * m + 4), w("tlx", t, t + 32, st=16))
+
+    def last_places():
+        gr = w("grow", 32, 64)
+        pick(gr, mapw(7), w("off", 14, 16))
+        turn(w("tlx", 256, 288), gr)
+
+    def lists(buf, c0, b, qs):
+        for a in range(4):
+            copy(w(buf, 32 * a, 32 * a + 32, 32 * b, 32 * b + 32), w("gc", c0 + 32 * b, c0 + 32 * b + 32, 32 * a, 32 * a + 32), qs[a])
+
+    def hops(extra=None):
+        for m in range(8):
+            hop(m)
+            if extra and m in extra:
+                extra[m]()
+            if m % 2:
+                lists("rt", 16, m // 2, "ssss" if m < 7 else "vsvs")
+        turn(w("tt"), w("rt"))
+        copy(w("offm"), w("tt", 0, 128, st=16))
+
+    def unpack(r):
+        for b in range(4):
+            mm("pa%d" % b, 256, "qe", 128 * b, "qx%d" % r)
+
+    def unpacked(b, q):
+        copy(w("win%d" % b, 0, 256), w("pa%d" % b, 0, 256), q)
+
+    def first():
+        quant("qx0", "xt", 0, 256)
+        for b in range(4):
+            quant("qe", "zt", 128 * b, 128, 3 - b)
+        unpack(0)
+        pick(mapw(3), w("it"), w("offa", 48, 64))
+
+    def second():
+        pick(mapw(6), w("it"), w("offa", 96, 112))
+
+    def third():
+        for b in range(4):
+            unpacked(b, "v")
+    hops({2: first, 5: second, 7: third})
+    far = (rank + 4) % N
+    for nm in ("", "_s"):
+        send(far, w("qw" + nm), w("qwl" + nm), "aw")
+    expect(far, [w("qwl"), w("qwl_s")], "aw")
+
+    def precompute_lists():
+        for b in range(4):
+            lists("rte", 0, b, "ssss")
+        turn(w("tte"), w("rte"))
+        copy(w("offe"), w("tte", 0, 128, st=16))
+        pick(w("cr"), w("cw"), w("offe"))
+        turn(w("ctr"), w("cr"))
+
+    def precompute_keys():
+        for b in range(4):
+            for a in range(4):
+                copy(w("c32", 8 * a, 8 * a + 8, 32 * b, 32 * b + 32), w("ctr", 32 * b, 32 * b + 32, 32 * a, 32 * a + 32, st=4), "vs"[a % 2])
+        ts(w("e8"), w("tlx", 0, 256, st=32), UNIT, None, A.mult)
+        for k in range(4):
+            tt(w("k1", k, 32, st=4), w("c32", k, 32, st=4), w("e8"), A.add)
+            tt(w("eq", k, 32, st=4), w("c32", k, 32, st=4), w("tlx", 32, 288, st=32), A.is_equal)
+        tt(w("k1"), w("k1"), w("g32"), A.add)
+        ts(w("eq"), w("eq"), 2.0 * P21, None, A.mult)
+        tt(w("key"), w("k1"), w("eq"), A.add)
+
+    def layer(src, c0, dst, d0, lay, qs="svsv"):
+        for b in range(4):
+            mm("pb%d" % b, 128, lay, 128 * b, src, c0)
+        for b in range(4):
+            o, i = w("ht", b, 512, st=4), w("pb%d" % b, 0, 128)
+            if qs[b] == "s":
+                op("s", lambda: g.scalar.activation(o[0], i[0], F.Relu, scale=0.03125), [o], [i])
+            else:
+                ts(o, i, 0.0, 0.03125, A.max, A.mult)
+        quant(dst, "ht", d0)
+
+    def repair():
+        ts(w("fl"), w("pb0", 0, 64), 0.0, None, A.is_gt)
+        tt(w("wp"), w("fl"), w("sig"), A.mult)
+        tt(w("u1"), w("wp", 0, 32), w("key"), A.add)
+        tt(w("uu", 0, 32), w("u1"), w("wp", 32, 64), A.add)
+        R, V1, VF, EF, LO = w("rr", 0, 1), w("rr", 1, 2), w("rr", 2, 3), w("e32", 0, 1), w("l32", 31, 32)
+        o, i = R, w("uu", 0, 33)
+        op("v", lambda: g.vector.tensor_reduce(o[0], i[0], AxisListType.X, A.min), [o], [i])
+        ts(w("e32"), w("cu"), R, ROUND, A.mult, A.add)
+        turn(w("t1"), w("e32"))
+        ts(V1, EF, -ROUND, -UNIT, A.add, A.mult)
+        ts(w("m32"), w("t1"), EF, None, A.is_equal)
+        tt(VF, V1, R, A.add)
+        ts(w("d32"), w("e32"), -1.0, TJC, A.mult, A.add)
+        scan(w("l32"), w("m32"), w("tri"))
+        ts(w("x64", 32, 64), w("cu"), UNIT, VF, A.mult, A.mult)
+        ts(w("x64", 0, 32), w("d32"), LO, EF, A.mult, A.add)
+        turn(w("t64"), w("x64"))
+        pick(w("p64"), w("t64"), w("oo", 0, 4))
+        for i in range(8):
+            a, b = 2 * (i // 4) + i % 2, 2 * (i // 4) + i // 2 % 2
+            copy(w("row", 64 * a, 64 * a + 64, 32 * b, 32 * b + 32), w("p64", 0, 64, 32 * a, 32 * a + 32), "vsvvsvsv"[i])
+        copy(w("row", 0, 128, 64, 128), w("row", 0, 128, 0, 64), "v")
+        copy(w("row", 128, 256, 0, 64), w("row", 128, 256, 64, 128), "s")
+        turn(w("t2"), w("row"))
+        for s in range(2):
+            ts(w("offr", s, 8, st=2), w("t2", 16 * s, 256, st=64), -ROUND, None, A.add)
+        for b in range(4):
+            scatter(w("map"), w("offr", 2 * b, 2 * b + 2), w("row", 64 * b + 32, 64 * b + 64))
+
+    def newest():
+        pick(w("brow"), w("it"), w("offm"), "s")
+        a8 = w("tt", 0, 128, st=16)
+        ts(w("fi"), a8, -7.5, 0.0625, A.add, A.mult)
+        ts(w("p1"), w("fi"), 16.0, H16, A.mult, A.add)
+        tt(w("p2"), w("p1"), a8, A.add)
+        tt(w("e128"), w("tt"), w("brow"), A.is_equal)
+        scan(w("sc"), w("e128"), w("kk"))
+        tt(w("p3"), w("p2"), w("sc", 15, 128, st=16), A.max)
+        copy(w("offi", 0, 16, st=2), w("p3"))
+        for c in range(8):
+            scatter(w("inv"), w("offi", 2 * c, 2 * c + 1), w("sl", 16 * c, 16 * c + 16))
+        turn(w("t512"), w("inv", 0, 512))
+        tt(w("n16"), w("t512", 0, 512, st=32), w("t512", 16, 512, st=32), A.max)
+        ts(w("noff"), w("n16"), 256.0, None, A.add)
+
+    def renew(r):
+        for b in (2, 3):
+            pick(w("oth", 256 * b - 512, 256 * b - 256), w("win%d" % b), w("noff"), "s")
+        for b in (0, 1):
+            o, wn, nf, fw = w("nx", b, 1024, st=4), w("win%d" % b), w("noff"), w("fh", 256 * b, 256 * b + 256)
+            op("v", lambda: g.vector.tensor_tensor(o[0], wn[0].indirect(nf[0]), fw[0], A.add), [o], [wn, nf, fw])
+        for b in (2, 3):
+            tt(w("nx", b, 1024, st=4), w("oth", 256 * b - 512, 256 * b - 256), w("pa%d" % b, 0, 256), A.add)
+        quant("qx%d" % (r + 1), "nx", 0, 256)
+
+    for r in range(3):
+        donor, asker = (rank + STEP[r]) % N, (rank - STEP[r]) % N
+        c0 = 128 * r
+        for b in range(4):
+            if r:
+                unpacked(b, "svsv"[b])
+            pick(w("mt", b, 512, st=4), w("win%d" % b, 0, 256), w("offm"), "svsv"[b], 2.0)
+        quant("qm", "mt", c0)
+        if r < 2:
+            for nm in ("", "_s"):
+                send(donor, w("qm" + nm, c0, c0 + 128), w("qml" + nm, c0, c0 + 128), "am%d" % r)
+            expect(asker, [w("qml", c0, c0 + 128), w("qml_s", c0, c0 + 128)], "am%d" % r)
+            if r == 0:
+                last_places()
+                late_constants()
+            else:
+                copy(w("inv", 0, 512), w("cini"), "s")
+                precompute_lists()
+            layer("qml", c0, "qh", c0, "qw")
+            for nm in ("", "_s"):
+                send(asker, w("qh" + nm, c0, c0 + 128), w("qx%d" % r + nm, 256, 384), "ah%d" % r)
+            expect(donor, [w("qx%d" % r, 256, 384), w("qx%d_s" % r, 256, 384)], "ah%d" % r)
+            if r == 0:
+                candidates()
+                precompute_lists()
+                copy(w("inv", 0, 512), w("cini"), "s")
+        else:
+            precompute_lists()
+            layer("qm", c0, "qx2", 256, "qwl")
+            copy(w("inv", 0, 512), w("cini"), "s")
+        precompute_keys()
+        mm("pb0", 128, "qx%d" % r, 256, "qup")
+        for b in range(4):
+            mm("pa%d" % b, 384, "qe", 128 * b, "qx%d" % r)
+        for b in range(4):
+            copy(w("win%d" % b, 256, 384), w("pa%d" % b, 256, 384), "s")
+            if b < 2:
+                copy(w("fh", 256 * b, 256 * b + 256), w("pa%d" % b, 0, 256), "s")
+        repair()
+        if r == 2:
+            dma("y", T.fo[:], T.map[0:1, 0:2048], [w("map", 0, 2048)], ())
+        hops()
+        newest()
+        if r < 2:
+            last_places()
+        renew(r)
+        if r < 2:
+            unpack(r + 1)
+    dma("y", T.oc[:], T.qx3[:, 0:256].bitcast(dt.uint8), [w("qx3", 0, 256)], ())
+    for k in range(4):
+        dma("s", T.osc[4 * k:4 * k + 4, :], T.qx3_s[32 * k:32 * k + 4, 0:256], [w("qx3_s", 0, 256)], ())
+    mm("pb1", 256, "qv", 0, "qx3")
+    copy(w("yt"), w("pb1", 0, 256))
+    dma("y", T.y[:], T.yt[:], [w("yt")], ())
+    for sem, n in count.items():
+        if known["g"].get(sem, 0) < n:
+            g.wait_ge(T.sem[sem], n)

@@ -22,23 +22,22 @@ def _mx(name, n):
 for _b in range(4):
     SCRATCH["pa%d" % _b] = ("psum", [128, 512], "float32")
     SCRATCH["pb%d" % _b] = ("psum", [128, 512], "float32")
-    _sb("win%d" % _b, 384, "bfloat16")
+    _sb("win%d" % _b, 512, "bfloat16")
     _mx("qx%d" % _b, 384)
 for _n, _k in [("qe", 512), ("qm", 384), ("qml", 256), ("qh", 256), ("qw", 512), ("qwl", 512), ("qu", 128), ("qup", 128), ("qv", 128)]:
     _mx(_n, _k)
 for _n, _k in [("oth", 512), ("fh", 512), ("xt", 1024), ("ut", 512), ("vt", 512), ("mt", 512), ("ht", 512), ("nx", 1024), ("zt", 528), ("zs", 528),
-               ("cini", 512), ("itz", 272), ("sl", 128), ("inv", 544), ("t512", 512)]:
+               ("cini", 512), ("itz", 256), ("sl", 128), ("inv", 640), ("t512", 512)]:
     _sb(_n, _k, "bfloat16")
-for _n, _k in [("offa", 128), ("aro", 64), ("off", 18), ("offm", 8), ("offe", 8), ("offr", 8), ("oo", 8), ("ul", 8), ("offi", 16), ("noff", 16), ("cil", 32)]:
+for _n, _k in [("offa", 128), ("aro", 64), ("off", 18), ("offm", 8), ("offe", 8), ("offr", 8), ("oo", 8), ("ul", 8), ("offi", 8), ("noff", 16), ("cil", 32)]:
     _sb(_n, _k, "uint16")
 for _n, _k in [("mpa", 128), ("ari", 64), ("ci8", 8), ("fi", 8)]:
     _sb(_n, _k, "int32")
-for _n, _k in [("ra", 1024), ("it", 256), ("map", 2304), ("cw", 256), ("cwa", 256), ("cf", 32), ("tlx", 288), ("gc", 144), ("grow", 64), ("rt", 128), ("tt", 128),
-               ("rte", 128), ("tte", 128), ("cr", 128), ("ctr", 128), ("c32", 32), ("e8", 8), ("k1", 32), ("eq", 32), ("key", 32), ("g32", 32), ("kab", 64),
-               ("sig", 64), ("gi", 32), ("fl", 64), ("wp", 64), ("u1", 32), ("uu", 40), ("rr", 8), ("cu", 32), ("x64", 64), ("d32", 32), ("t1", 32), ("e32", 32),
-               ("m32", 32), ("l32", 32), ("t64", 64), ("p64", 64), ("row", 256), ("t2", 256), ("oof", 16), ("ulf", 8), ("tri", 32), ("i32", 32), ("kk", 128),
-               ("ki", 128), ("v32", 32), ("h32", 32), ("gc0", 16), ("brow", 128), ("e128", 128), ("sc", 128), ("p1", 8), ("p2", 8), ("p3", 8), ("n16", 16),
-               ("yt", 256)]:
+for _n, _k in [("ra", 1024), ("it", 256), ("map", 2304), ("cw", 256), ("cwa", 256), ("cf", 32), ("gc", 144), ("grow", 32), ("dg", 16), ("rt", 128), ("tt", 128),
+               ("rte", 128), ("tte", 128), ("cr", 128), ("ctr", 128), ("c32", 32), ("e8", 8), ("lw", 8), ("k1", 32), ("eq", 32), ("kb4", 132), ("kbs", 132),
+               ("ktri", 132), ("gi", 8), ("w8", 8), ("rr", 8), ("cu", 32), ("x64", 64), ("d32", 32), ("t1", 32), ("e32", 32),
+               ("m32", 32), ("l32", 32), ("t64", 64), ("p64", 64), ("row", 256), ("t2", 256), ("oof", 16), ("ulf", 8), ("tri", 32), ("i32", 32), ("kk", 768),
+               ("ki", 768), ("ee", 768), ("sc", 768), ("v32", 32), ("h32", 32), ("gc0", 16), ("brow", 128), ("p1", 8), ("p2", 8), ("yt", 256)]:
     _sb(_n, _k)
 
 CODES = {n for n, s in SCRATCH.items() if s[2] == "float8_e4m3fn_x4"}
@@ -211,19 +210,25 @@ def rank_program(g, core, T, topo):
     iota(w("gc0"), [[-1, 16]], 127, -1)
     iota(w("it"), [[1, 256]], 0, 0)
     iota(w("i32"), [[1, 32]], 0, 0)
-    iota(w("kab", 0, 32), [[0, 8], [1, 2], [0, 2]], 0, 0)
-    iota(w("kab", 32, 64), [[0, 16], [1, 2]], 0, 0)
     fill(w("zs"), 0.5)
     fill(w("cu"), 1.0 / UNIT)
     z = w("zt", 0, 516)
     zs = w("zs", 0, 516)
     op("g", lambda: g.affine_select(z[0], zs[0], [[-1, 516]], A.is_equal, 0.0, 3, 4), [z], [zs])
-    iota(w("gi"), [[1, 8], [0, 4]], 0, 0)
-    iota(w("ki"), [[0, 8], [1, 16]], 0, 0)
-    iota(w("v32"), [[16, 16], [0, 2]], -256, 0)
+    iota(w("gi"), [[1, 8]], 0, 0)
+    iota(w("w8"), [[16, 8]], 512, 0)
+    iota(w("ktri"), [[0, 33], [1, 4]], 0, 0)
+    iota(w("v32"), [[16, 16], [0, 2]], 0, 0)
     iota(w("h32"), [[0, 16], [1, 2]], 0, 0)
-    iota(w("sl"), [[1, 128]], 0, 0)
-    iota(w("itz", 0, 256), [[1, 256]], -256, 0)
+    iota(w("sl"), [[2, 128]], 256, 0)
+    iota(w("itz"), [[1, 256]], 0, 0)
+
+    def late_iotas():
+        iota(w("ki", 0, 512), [[-16, 4], [1, 128]], 0, 0)
+        iota(w("ki", 512, 768), [[-16, 4], [1, 64]], 0, 0)
+        iota(w("ee"), [[0, 768]], 0, 0)
+        for b in range(4):
+            iota(w("win%d" % b, 256, 512), [[0, 256]], 0, 0)
 
     def bits(c, sh, m):
         o, i = w("ci8", c, c + 1), w("ci8", 0, 1)
@@ -235,59 +240,58 @@ def rank_program(g, core, T, topo):
     bits(2, 4, 1)
     bits(3, 0, 31)
     bits(4, 2, 3)
-    copy(w("cf", 0, 5), w("ci8", 0, 5))
+    bits(5, 1, 7)
+    copy(w("cf", 0, 6), w("ci8", 0, 6))
 
     def cf(c):
         return w("cf", c, c + 1)
-    PP, QQ, HH, II, KR, H16, TQ, TJ, TJC = [cf(c) for c in range(9)]
+    PP, QQ, HH, II, KR, Q2, H16, TJ, TJC, NQ = [cf(c) for c in range(10)]
     MK = [cf(12 + k) for k in range(4)]
-    ts(w("tlx", 0, 1), PP, -1.0, 127.0, A.mult, A.add)
-    ts(cf(10), HH, 32.0, -16.0, A.mult, A.add)
-    tt(w("tlx", 16, 17), w("tlx", 0, 1), cf(10), A.add)
-    copy(w("off", 0, 2), w("tlx", 0, 32, st=16))
+    ts(w("off", 0, 1), PP, -1.0, 127.0, A.mult, A.add)
+    ts(w("dg"), w("i32", 0, 16), QQ, None, A.is_equal)
     ts(H16, HH, 16.0, None, A.mult)
     ts(w("gc", 0, 16), w("gc0"), QQ, None, A.add)
-    ts(TQ, QQ, 512.0, None, A.add)
+    ts(w("tri"), w("i32"), II, None, A.is_gt)
     ts(TJ, PP, 2048.0, None, A.add)
-    ts(TJC, TJ, ROUND, None, A.add)
-    ts(w("uu", 32, 33), TJ, UNIT, None, A.mult)
     for k in range(4):
         ts(MK[k], KR, float(k), None, A.is_equal)
+    ts(TJC, TJ, ROUND, None, A.add)
+    ts(NQ, QQ, -1.0, -0.5, A.mult, A.add)
     ts(w("oof", 0, 1), QQ, H16, None, A.add)
     ts(cf(11), QQ, 16.0, None, A.add)
     tt(w("oof", 1, 2), cf(11), H16, A.subtract)
     ts(w("oof", 2, 4), w("oof", 0, 2), 32.0, None, A.add)
     copy(w("oo", 0, 4), w("oof", 0, 4))
-    fill(w("ulf"), 0.0)
-    ts(w("ulf", 0, 1), KR, 16.0, None, A.mult)
-    ts(w("ulf", 1, 2), KR, 16.0, 64.0, A.mult, A.add)
-    ts(w("ulf", 2, 4), w("ulf", 0, 2), 1.0, None, A.add)
-    copy(w("ul"), w("ulf"))
 
     def late_constants():
-        ts(w("tri"), w("i32"), II, None, A.is_gt)
-        ts(w("sig"), w("kab"), -2.0 * P21, P21, A.mult, A.add)
-        tt(w("g32"), w("kab", 0, 32), w("kab", 32, 64), A.add)
-        ts(w("g32"), w("g32"), P21, None, A.mult)
+        fill(w("ulf"), 0.0)
+        ts(w("ktri"), w("ktri"), 3.0, None, A.is_lt)
         ts(w("gi"), w("gi"), 256.0 * UNIT, None, A.mult)
-        tt(w("g32"), w("g32"), w("gi"), A.add)
-        ts(w("kk"), w("ki"), QQ, None, A.is_gt)
-        ts(w("kk", 15, 128, st=16), w("kk", 15, 128, st=16), TQ, None, A.mult)
+        for c in range(4):
+            ts(w("ulf", c, c + 1), Q2, 16.0, float(c // 2), A.mult, A.add)
+        fill(w("kb4"), 0.0)
+        copy(w("ul"), w("ulf"))
+        o, i, n = w("ki"), w("ki"), NQ
+        op("s", lambda: g.scalar.activation(o[0], i[0], F.Sign, bias=n[0]), [o], [i, n])
+        o3 = w("kk")
+        op("s", lambda: g.scalar.activation(o3[0], i[0], F.Relu), [o3], [i])
+        ts(w("w8"), w("w8"), QQ, None, A.add)
         ts(w("h32"), w("h32"), HH, None, A.is_equal)
         ts(w("v32"), w("v32"), QQ, None, A.add)
+        tt(w("kk", 127, 512, st=128), w("kk", 127, 512, st=128), w("w8", 0, 4), A.mult)
         tt(w("v32"), w("v32"), w("h32"), A.mult)
-        ts(w("cil"), w("v32"), 256.0, None, A.add)
-        fill(w("itz", 256, 272), -256.0)
+        tt(w("kk", 575, 768, st=64), w("kk", 575, 768, st=64), w("w8", 4, 8), A.mult)
+        copy(w("cil"), w("v32"))
+        ts(w("kb4", 128, 129), TJ, UNIT, None, A.mult)
         pick(w("cini"), w("itz"), w("cil"), "s")
         quant("qu", "ut")
         quant("qv", "vt")
-        o, i, l = w("qup"), w("qu"), w("ul")
-        op("v", lambda: g.vector.tensor_copy(o[0].bitcast(dt.uint32), i[0].bitcast(dt.uint32).indirect(l[0])), [o], [i, l])
+        o4, i4, l = w("qup"), w("qu"), w("ul")
+        op("v", lambda: g.vector.tensor_copy(o4[0].bitcast(dt.uint32), i4[0].bitcast(dt.uint32).indirect(l[0])), [o4], [i4, l])
         o2, i2 = w("qup_s"), w("qu_s")
         op("v", lambda: g.vector.tensor_copy(o2[0], i2[0].indirect(l[0])), [o2], [i2, l])
 
     def candidates():
-        copy(w("aro"), w("ari"))
         for k in range(4):
             pick(w("ra", 256 * k, 256 * k + 256), w("it"), w("aro", 16 * k, 16 * k + 16), "s", MK[k])
         tt(w("cw"), w("ra", 0, 256), w("ra", 256, 512), A.add)
@@ -303,34 +307,36 @@ def rank_program(g, core, T, topo):
         if m not in (3, 6):
             pick(mapw(m), w("it"), w("offa", 16 * m, 16 * m + 16), "v" if m == 0 else "s")
 
-    def hop(m):
-        gr = w("grow", 32 * (m % 2), 32 * (m % 2) + 32)
-        gc = w("gc", 16 * m + 16, 16 * m + 32)
-        t = 32 * m + 32
-        if m == 7:
-            pick(gc, mapw(m), w("off", 2 * m, 2 * m + 1))
-            return
-        pick(gr, mapw(m), w("off", 2 * m, 2 * m + 2))
-        pick(gc, mapw(m), w("off", 2 * m, 2 * m + 1), "s")
-        turn(w("tlx", t, t + 32), gr)
-        copy(w("off", 2 * m + 2, 2 * m + 4), w("tlx", t, t + 32, st=16))
+    def step1(m):
+        gr, mp, of, dg = w("grow", 16 * (m % 2), 16 * (m % 2) + 16), mapw(m), w("off", 2 * m, 2 * m + 1), w("dg")
+        op("v", lambda: g.vector.tensor_tensor(gr[0], mp[0].indirect(of[0]), dg[0], A.mult), [gr], [mp, of, dg])
 
-    def last_places():
-        gr = w("grow", 32, 64)
-        pick(gr, mapw(7), w("off", 14, 16))
-        turn(w("tlx", 256, 288), gr)
+    def step2(m):
+        o, i = w("off", 2 * m + 2, 2 * m + 3), w("grow", 16 * (m % 2), 16 * (m % 2) + 16)
+        op("v", lambda: g.vector.tensor_reduce(o[0], i[0], AxisListType.X, A.max), [o], [i])
+
+    def hop(m, extra):
+        gc = w("gc", 16 * m + 16, 16 * m + 32)
+        pick(gc, mapw(m), w("off", 2 * m, 2 * m + 1), "v" if m == 7 else "s")
+        if m < 7:
+            step1(m)
+            if extra:
+                extra.pop(0)()
+            step2(m)
+        if extra:
+            extra.pop(0)()
 
     def lists(buf, c0, b, qs):
         for a in range(4):
             copy(w(buf, 32 * a, 32 * a + 32, 32 * b, 32 * b + 32), w("gc", c0 + 32 * b, c0 + 32 * b + 32, 32 * a, 32 * a + 32), qs[a])
 
-    def hops(extra=None):
+    def hops(extra=None, places=False):
         for m in range(8):
-            hop(m)
-            if extra and m in extra:
-                extra[m]()
+            hop(m, extra)
             if m % 2:
                 lists("rt", 16, m // 2, "ssss" if m < 7 else "vsvs")
+            if places and m in (0, 2, 4, 7):
+                lists("rte", 0, (m + 1) // 2 - m // 7, "ssss")
         turn(w("tt"), w("rt"))
         copy(w("offm"), w("tt", 0, 128, st=16))
 
@@ -341,44 +347,36 @@ def rank_program(g, core, T, topo):
     def unpacked(b, q):
         copy(w("win%d" % b, 0, 256), w("pa%d" % b, 0, 256), q)
 
-    def first():
-        quant("qx0", "xt", 0, 256)
-        for b in range(4):
-            quant("qe", "zt", 128 * b, 128, 3 - b)
-        unpack(0)
-        pick(mapw(3), w("it"), w("offa", 48, 64))
-
-    def second():
-        pick(mapw(6), w("it"), w("offa", 96, 112))
-
-    def third():
-        for b in range(4):
-            unpacked(b, "v")
-    hops({2: first, 5: second, 7: third})
+    def constant(b):
+        quant("qe", "zt", 128 * b, 128, 3 - b)
+    hops([lambda: constant(0), lambda: pick(mapw(3), w("it"), w("offa", 48, 64)), lambda: constant(1), lambda: constant(2), lambda: constant(3),
+          lambda: quant("qx0", "xt", 0, 256), lambda: (unpack(0), pick(mapw(6), w("it"), w("offa", 96, 112))), lambda: copy(w("aro"), w("ari")),
+          lambda: None, lambda: unpacked(0, "v"), lambda: unpacked(1, "v"), lambda: unpacked(2, "v"), lambda: unpacked(3, "v")])
     far = (rank + 4) % N
     for nm in ("", "_s"):
         send(far, w("qw" + nm), w("qwl" + nm), "aw")
     expect(far, [w("qwl"), w("qwl_s")], "aw")
+    late_iotas()
 
-    def precompute_lists():
-        for b in range(4):
-            lists("rte", 0, b, "ssss")
-        turn(w("tte"), w("rte"))
-        copy(w("offe"), w("tte", 0, 128, st=16))
-        pick(w("cr"), w("cw"), w("offe"))
-        turn(w("ctr"), w("cr"))
+    def requests():
+        def cells(a):
+            for b in range(4):
+                copy(w("c32", 8 * a, 8 * a + 8, 32 * b, 32 * b + 32), w("ctr", 32 * b, 32 * b + 32, 32 * a, 32 * a + 32, st=4), "vsvs"[b])
 
-    def precompute_keys():
-        for b in range(4):
-            for a in range(4):
-                copy(w("c32", 8 * a, 8 * a + 8, 32 * b, 32 * b + 32), w("ctr", 32 * b, 32 * b + 32, 32 * a, 32 * a + 32, st=4), "vs"[a % 2])
-        ts(w("e8"), w("tlx", 0, 256, st=32), UNIT, None, A.mult)
-        for k in range(4):
+        def sums(k):
             tt(w("k1", k, 32, st=4), w("c32", k, 32, st=4), w("e8"), A.add)
-            tt(w("eq", k, 32, st=4), w("c32", k, 32, st=4), w("tlx", 32, 288, st=32), A.is_equal)
-        tt(w("k1"), w("k1"), w("g32"), A.add)
-        ts(w("eq"), w("eq"), 2.0 * P21, None, A.mult)
-        tt(w("key"), w("k1"), w("eq"), A.add)
+            tt(w("eq", k, 32, st=4), w("c32", k, 32, st=4), w("lw"), A.is_equal)
+
+        def keys(k):
+            s = 4 * (16 * (k // 2) + k % 2)
+            tt(w("kb4", s, s + 64, st=8), w("k1", k, 32, st=4), w("eq", k, 32, st=4), A.max)
+        return [lambda: step1(7), lambda: turn(w("tte"), w("rte")), lambda: step2(7), lambda: copy(w("offe"), w("tte", 0, 128, st=16)),
+                lambda: ts(w("e8"), w("off", 0, 16, st=2), UNIT, None, A.mult),
+                lambda: (pick(w("cr"), w("cw"), w("offe")), copy(w("lw"), w("off", 2, 18, st=2))),
+                lambda: tt(w("e8"), w("e8"), w("gi"), A.add),
+                lambda: turn(w("ctr"), w("cr")), lambda: (cells(0), cells(1)), lambda: (cells(2), cells(3)),
+                lambda: (sums(0), sums(1)), lambda: (sums(2), sums(3)), lambda: ts(w("eq"), w("eq"), P21, None, A.mult),
+                lambda: (keys(0), keys(1), keys(2), keys(3))]
 
     def layer(src, c0, dst, d0, lay, qs="svsv"):
         for b in range(4):
@@ -392,12 +390,13 @@ def rank_program(g, core, T, topo):
         quant(dst, "ht", d0)
 
     def repair():
-        ts(w("fl"), w("pb0", 0, 64), 0.0, None, A.is_gt)
-        tt(w("wp"), w("fl"), w("sig"), A.mult)
-        tt(w("u1"), w("wp", 0, 32), w("key"), A.add)
-        tt(w("uu", 0, 32), w("u1"), w("wp", 32, 64), A.add)
+        ts(w("kb4", 1, 64, st=4), w("pb0", 0, 16), 0.0, P21, A.is_gt, A.mult)
+        ts(w("kb4", 65, 128, st=4), w("pb0", 16, 32), 0.0, P21, A.is_le, A.mult)
+        ts(w("kb4", 2, 128, st=8), w("pb0", 32, 64, st=2), 0.0, P21, A.is_gt, A.mult)
+        ts(w("kb4", 6, 128, st=8), w("pb0", 33, 64, st=2), 0.0, P21, A.is_le, A.mult)
+        scan(w("kbs"), w("kb4"), w("ktri"))
         R, V1, VF, EF, LO = w("rr", 0, 1), w("rr", 1, 2), w("rr", 2, 3), w("e32", 0, 1), w("l32", 31, 32)
-        o, i = R, w("uu", 0, 33)
+        o, i = R, w("kbs", 2, 132, st=4)
         op("v", lambda: g.vector.tensor_reduce(o[0], i[0], AxisListType.X, A.min), [o], [i])
         ts(w("e32"), w("cu"), R, ROUND, A.mult, A.add)
         turn(w("t1"), w("e32"))
@@ -421,21 +420,38 @@ def rank_program(g, core, T, topo):
         for b in range(4):
             scatter(w("map"), w("offr", 2 * b, 2 * b + 2), w("row", 64 * b + 32, 64 * b + 64))
 
-    def newest():
+    def newest(fillers):
+        def filler(n=1):
+            for _ in range(n):
+                if fillers:
+                    fillers.pop(0)()
+
+        def same(c):
+            s = 144 * c if c < 4 else 512 + 80 * (c - 4)
+            ts(w("ee", s, s + 128 - 16 * c), w("brow", 16 * c, 128), w("tt", 16 * c, 16 * c + 1), None, A.is_equal)
         pick(w("brow"), w("it"), w("offm"), "s")
         a8 = w("tt", 0, 128, st=16)
         ts(w("fi"), a8, -7.5, 0.0625, A.add, A.mult)
+        filler(2)
         ts(w("p1"), w("fi"), 16.0, H16, A.mult, A.add)
+        filler(2)
+        for c in range(4):
+            same(c)
         tt(w("p2"), w("p1"), a8, A.add)
-        tt(w("e128"), w("tt"), w("brow"), A.is_equal)
-        scan(w("sc"), w("e128"), w("kk"))
-        tt(w("p3"), w("p2"), w("sc", 15, 128, st=16), A.max)
-        copy(w("offi", 0, 16, st=2), w("p3"))
-        for c in range(8):
-            scatter(w("inv"), w("offi", 2 * c, 2 * c + 1), w("sl", 16 * c, 16 * c + 16))
+        for c in range(4, 8):
+            same(c)
+        filler()
+        scan(w("sc"), w("ee"), w("kk"))
+        filler()
+        tt(w("offi", 0, 4), w("p2", 0, 4), w("sc", 127, 512, st=128), A.max)
+        tt(w("offi", 4, 8), w("p2", 4, 8), w("sc", 575, 768, st=64), A.max)
+        filler()
+        scatter(w("inv"), w("offi"), w("sl"))
+        filler()
         turn(w("t512"), w("inv", 0, 512))
-        tt(w("n16"), w("t512", 0, 512, st=32), w("t512", 16, 512, st=32), A.max)
-        ts(w("noff"), w("n16"), 256.0, None, A.add)
+        filler()
+        tt(w("noff"), w("t512", 0, 512, st=32), w("t512", 16, 512, st=32), A.max)
+        filler()
 
     def renew(r):
         for b in (2, 3):
@@ -447,6 +463,7 @@ def rank_program(g, core, T, topo):
             tt(w("nx", b, 1024, st=4), w("oth", 256 * b - 512, 256 * b - 256), w("pa%d" % b, 0, 256), A.add)
         quant("qx%d" % (r + 1), "nx", 0, 256)
 
+    pieces = []
     for r in range(3):
         donor, asker = (rank + STEP[r]) % N, (rank - STEP[r]) % N
         c0 = 128 * r
@@ -460,40 +477,41 @@ def rank_program(g, core, T, topo):
                 send(donor, w("qm" + nm, c0, c0 + 128), w("qml" + nm, c0, c0 + 128), "am%d" % r)
             expect(asker, [w("qml", c0, c0 + 128), w("qml_s", c0, c0 + 128)], "am%d" % r)
             if r == 0:
-                last_places()
+                candidates()
                 late_constants()
-            else:
-                copy(w("inv", 0, 512), w("cini"), "s")
-                precompute_lists()
+            while pieces:
+                pieces.pop(0)()
             layer("qml", c0, "qh", c0, "qw")
             for nm in ("", "_s"):
                 send(asker, w("qh" + nm, c0, c0 + 128), w("qx%d" % r + nm, 256, 384), "ah%d" % r)
             expect(donor, [w("qx%d" % r, 256, 384), w("qx%d_s" % r, 256, 384)], "ah%d" % r)
             if r == 0:
-                candidates()
-                precompute_lists()
-                copy(w("inv", 0, 512), w("cini"), "s")
+                for b in range(4):
+                    lists("rte", 0, b, "ssss")
+                for piece in requests():
+                    piece()
         else:
-            precompute_lists()
             layer("qm", c0, "qx2", 256, "qwl")
-            copy(w("inv", 0, 512), w("cini"), "s")
-        precompute_keys()
+            while pieces:
+                pieces.pop(0)()
+        copy(w("inv", 0, 512), w("cini"), "s")
         mm("pb0", 128, "qx%d" % r, 256, "qup")
         for b in range(4):
             mm("pa%d" % b, 384, "qe", 128 * b, "qx%d" % r)
         for b in range(4):
-            copy(w("win%d" % b, 256, 384), w("pa%d" % b, 256, 384), "s")
+            copy(w("win%d" % b, 256, 512, st=2), w("pa%d" % b, 256, 384), "s")
             if b < 2:
                 copy(w("fh", 256 * b, 256 * b + 256), w("pa%d" % b, 0, 256), "s")
         repair()
         if r == 2:
             dma("y", T.fo[:], T.map[0:1, 0:2048], [w("map", 0, 2048)], ())
-        hops()
-        newest()
-        if r < 2:
-            last_places()
+        hops(places=r < 2)
+        pieces = requests() if r < 2 else []
+        newest(pieces)
         renew(r)
         if r < 2:
+            if pieces:
+                pieces.pop(0)()
             unpack(r + 1)
     dma("y", T.oc[:], T.qx3[:, 0:256].bitcast(dt.uint8), [w("qx3", 0, 256)], ())
     for k in range(4):

@@ -1,4 +1,4 @@
-from concourse.bass import DstId, RemoteDMATransfer
+import math
 from concourse.mybir import dt, AluOpType as A, AxisListType, ActivationFunctionType as F
 
 N = 8
@@ -26,8 +26,8 @@ for _b in range(4):
     _mx("qx%d" % _b, 384)
 for _n, _k in [("qe", 512), ("qm", 384), ("qml", 256), ("qh", 256), ("qw", 512), ("qwl", 512), ("qu", 128), ("qup", 128), ("qv", 128)]:
     _mx(_n, _k)
-for _n, _k in [("oth", 512), ("fh", 512), ("xt", 1024), ("ut", 512), ("vt", 512), ("mt", 512), ("ht", 512), ("nx", 1024), ("zt", 528), ("zs", 528),
-               ("cini", 512), ("itz", 256), ("sl", 128), ("inv", 640), ("t512", 512)]:
+for _n, _k in [("xt", 1024), ("ut", 512), ("vt", 512), ("mt", 512), ("ht", 512), ("nx", 1024), ("zt", 528), ("zs", 528),
+               ("cini", 512), ("itz", 256), ("sl", 128), ("inv", 1024), ("t512", 512), ("kk", 768), ("ee", 768), ("sc", 768), ("brow", 128)]:
     _sb(_n, _k, "bfloat16")
 for _n, _k in [("offa", 128), ("aro", 64), ("off", 18), ("offm", 8), ("offe", 8), ("offr", 8), ("oo", 8), ("ul", 8), ("offi", 8), ("noff", 16), ("cil", 32)]:
     _sb(_n, _k, "uint16")
@@ -36,8 +36,8 @@ for _n, _k in [("mpa", 128), ("ari", 64), ("ci8", 8), ("fi", 8)]:
 for _n, _k in [("ra", 1024), ("it", 256), ("map", 2304), ("cw", 256), ("cwa", 256), ("cf", 32), ("gc", 144), ("grow", 32), ("dg", 16), ("rt", 128), ("tt", 128),
                ("rte", 128), ("tte", 128), ("cr", 128), ("ctr", 128), ("c32", 32), ("e8", 8), ("lw", 8), ("k1", 32), ("eq", 32), ("kb4", 132), ("kbs", 132),
                ("ktri", 132), ("gi", 8), ("w8", 8), ("rr", 8), ("cu", 32), ("x64", 64), ("d32", 32), ("t1", 32), ("e32", 32),
-               ("m32", 32), ("l32", 32), ("t64", 64), ("p64", 64), ("row", 256), ("t2", 256), ("oof", 16), ("ulf", 8), ("tri", 32), ("i32", 32), ("kk", 768),
-               ("ki", 768), ("ee", 768), ("sc", 768), ("v32", 32), ("h32", 32), ("gc0", 16), ("brow", 128), ("p1", 8), ("p2", 8), ("yt", 256)]:
+               ("m32", 32), ("l32", 32), ("t64", 64), ("p64", 64), ("row", 256), ("t2", 256), ("oof", 16), ("ulf", 8), ("tri", 32), ("i32", 32),
+               ("ki", 768), ("dq", 512), ("fg", 512), ("v32", 32), ("h32", 32), ("gc0", 16), ("p1", 8), ("p2", 8), ("yt", 256)]:
     _sb(_n, _k)
 
 CODES = {n for n, s in SCRATCH.items() if s[2] == "float8_e4m3fn_x4"}
@@ -68,7 +68,7 @@ def rank_program(g, core, T, topo):
     def overlap(a, b):
         if a[2] >= b[3] or b[2] >= a[3] or a[4] >= b[5] or b[4] >= a[5]:
             return False
-        return not (a[6] == b[6] and a[6] > 1 and (a[4] - b[4]) % a[6])
+        return (a[4] - b[4]) % math.gcd(a[6], b[6]) == 0
 
     def covers(a, b):
         return a[2] <= b[2] and a[3] >= b[3] and a[4] <= b[4] and a[5] >= b[5] and (a[6] == 1 or (a[6] == b[6] and (a[4] - b[4]) % a[6] == 0))
@@ -130,12 +130,15 @@ def rank_program(g, core, T, topo):
         rid, pid, _ = topo.addr(dc)
         l = "l%d" % nl[0]
         nl[0] += 1
-        g.remote_dma(raw(dst), raw(src), T.sem[sem], T.sem[l], pid, rid, topo.mask(core, dc))
-        count[l] = len(topo.engines(core, dc))
+        g.remote_dma(raw(dst), raw(src), T.sem[sem], T.sem[l], pid, rid, sum(1 << e for e in engines(rank)))
+        count[l] = len(engines(rank))
         note("g", [src], [], l, count[l], False)
 
+    def engines(r):
+        return topo.engines(T.cores[r], T.cores[(r + 4) % N])
+
     def expect(frm, views, sem):
-        n = len(topo.engines(T.cores[frm], core)) * len(views)
+        n = len(engines(frm)) * len(views)
         count[sem] = n
         note("x", [], views, sem, n, False)
 
@@ -158,6 +161,9 @@ def rank_program(g, core, T, topo):
             op("s", lambda: g.scalar.activation(out[0], win[0].indirect(off[0]), F.Copy, scale=scale), [out], rd)
         else:
             op("s", lambda: g.scalar.activation(out[0], win[0].indirect(off[0]), F.Copy, scale=scale[0]), [out], rd + [scale])
+
+    def halve(out, in_):
+        op("s", lambda: g.scalar.activation(out[0], in_[0], F.Copy, scale=0.5), [out], [in_])
 
     def scatter(win, off, in_):
         op("v", lambda: g.vector.tensor_copy(win[0].indirect(off[0]), in_[0]), [win], [off, in_])
@@ -216,7 +222,7 @@ def rank_program(g, core, T, topo):
     zs = w("zs", 0, 516)
     op("g", lambda: g.affine_select(z[0], zs[0], [[-1, 516]], A.is_equal, 0.0, 3, 4), [z], [zs])
     iota(w("gi"), [[1, 8]], 0, 0)
-    iota(w("w8"), [[16, 8]], 512, 0)
+    iota(w("w8"), [[64, 8]], 512, 0)
     iota(w("ktri"), [[0, 33], [1, 4]], 0, 0)
     iota(w("v32"), [[16, 16], [0, 2]], 0, 0)
     iota(w("h32"), [[0, 16], [1, 2]], 0, 0)
@@ -257,6 +263,7 @@ def rank_program(g, core, T, topo):
         ts(MK[k], KR, float(k), None, A.is_equal)
     ts(TJC, TJ, ROUND, None, A.add)
     ts(NQ, QQ, -1.0, -0.5, A.mult, A.add)
+    ts(cf(10), QQ, 4.0, None, A.mult)
     ts(w("oof", 0, 1), QQ, H16, None, A.add)
     ts(cf(11), QQ, 16.0, None, A.add)
     tt(w("oof", 1, 2), cf(11), H16, A.subtract)
@@ -271,25 +278,28 @@ def rank_program(g, core, T, topo):
             ts(w("ulf", c, c + 1), Q2, 16.0, float(c // 2), A.mult, A.add)
         fill(w("kb4"), 0.0)
         copy(w("ul"), w("ulf"))
-        o, i, n = w("ki"), w("ki"), NQ
-        op("s", lambda: g.scalar.activation(o[0], i[0], F.Sign, bias=n[0]), [o], [i, n])
-        o3 = w("kk")
-        op("s", lambda: g.scalar.activation(o3[0], i[0], F.Relu), [o3], [i])
-        ts(w("w8"), w("w8"), QQ, None, A.add)
+        ts(w("w8"), w("w8"), cf(10), None, A.add)
         ts(w("h32"), w("h32"), HH, None, A.is_equal)
         ts(w("v32"), w("v32"), QQ, None, A.add)
-        tt(w("kk", 127, 512, st=128), w("kk", 127, 512, st=128), w("w8", 0, 4), A.mult)
+        quant("qu", "ut")
         tt(w("v32"), w("v32"), w("h32"), A.mult)
-        tt(w("kk", 575, 768, st=64), w("kk", 575, 768, st=64), w("w8", 4, 8), A.mult)
+        quant("qv", "vt")
         copy(w("cil"), w("v32"))
         ts(w("kb4", 128, 129), TJ, UNIT, None, A.mult)
-        pick(w("cini"), w("itz"), w("cil"), "s")
-        quant("qu", "ut")
-        quant("qv", "vt")
         o4, i4, l = w("qup"), w("qu"), w("ul")
         op("v", lambda: g.vector.tensor_copy(o4[0].bitcast(dt.uint32), i4[0].bitcast(dt.uint32).indirect(l[0])), [o4], [i4, l])
         o2, i2 = w("qup_s"), w("qu_s")
         op("v", lambda: g.vector.tensor_copy(o2[0], i2[0].indirect(l[0])), [o2], [i2, l])
+
+    def mask1():
+        o, i, n, o3 = w("ki"), w("ki"), NQ, w("kk")
+        op("s", lambda: g.scalar.activation(o[0], i[0], F.Sign, bias=n[0]), [o], [i, n])
+        op("s", lambda: g.scalar.activation(o3[0], i[0], F.Relu), [o3], [i])
+
+    def mask2():
+        tt(w("kk", 127, 512, st=128), w("kk", 127, 512, st=128), w("w8", 0, 4), A.mult)
+        tt(w("kk", 575, 768, st=64), w("kk", 575, 768, st=64), w("w8", 4, 8), A.mult)
+        pick(w("cini"), w("itz"), w("cil"), "s")
 
     def candidates():
         for k in range(4):
@@ -298,12 +308,14 @@ def rank_program(g, core, T, topo):
         tt(w("cwa"), w("ra", 512, 768), w("ra", 768, 1024), A.add)
         tt(w("cw"), w("cw"), w("cwa"), A.add)
 
-    for a in range(4):
-        copy(w("offa", 0, 128, 32 * a, 32 * a + 32), w("mpa", 0, 128, 0, 32))
-
     def mapw(m):
         return w("map", 256 * m, 256 * m + 256)
+    for a in range(4):
+        copy(w("offa", 0, 32, 32 * a, 32 * a + 32), w("mpa", 0, 32, 0, 32))
     for m in range(8):
+        if m == 1:
+            for a in range(4):
+                copy(w("offa", 32, 128, 32 * a, 32 * a + 32), w("mpa", 32, 128, 0, 32))
         if m not in (3, 6):
             pick(mapw(m), w("it"), w("offa", 16 * m, 16 * m + 16), "v" if m == 0 else "s")
 
@@ -371,11 +383,11 @@ def rank_program(g, core, T, topo):
             s = 4 * (16 * (k // 2) + k % 2)
             tt(w("kb4", s, s + 64, st=8), w("k1", k, 32, st=4), w("eq", k, 32, st=4), A.max)
         return [lambda: step1(7), lambda: turn(w("tte"), w("rte")), lambda: step2(7), lambda: copy(w("offe"), w("tte", 0, 128, st=16)),
-                lambda: ts(w("e8"), w("off", 0, 16, st=2), UNIT, None, A.mult),
-                lambda: (pick(w("cr"), w("cw"), w("offe")), copy(w("lw"), w("off", 2, 18, st=2))),
-                lambda: tt(w("e8"), w("e8"), w("gi"), A.add),
-                lambda: turn(w("ctr"), w("cr")), lambda: (cells(0), cells(1)), lambda: (cells(2), cells(3)),
-                lambda: (sums(0), sums(1)), lambda: (sums(2), sums(3)), lambda: ts(w("eq"), w("eq"), P21, None, A.mult),
+                lambda: pick(w("cr"), w("cw"), w("offe")),
+                lambda: (ts(w("e8"), w("off", 0, 16, st=2), UNIT, None, A.mult), turn(w("ctr"), w("cr")), copy(w("lw"), w("off", 2, 18, st=2))),
+                lambda: (tt(w("e8"), w("e8"), w("gi"), A.add), cells(0), cells(1)), lambda: (cells(2), cells(3)),
+                lambda: (sums(0), sums(1)), lambda: (sums(2), sums(3)),
+                lambda: ts(w("eq"), w("eq"), P21, None, A.mult),
                 lambda: (keys(0), keys(1), keys(2), keys(3))]
 
     def layer(src, c0, dst, d0, lay, qs="svsv"):
@@ -429,7 +441,12 @@ def rank_program(g, core, T, topo):
         def same(c):
             s = 144 * c if c < 4 else 512 + 80 * (c - 4)
             ts(w("ee", s, s + 128 - 16 * c), w("brow", 16 * c, 128), w("tt", 16 * c, 16 * c + 1), None, A.is_equal)
+        def mean(b):
+            s = slice(128 * b, 128 * b + 128)
+            tt(w("win%d" % b, 256, 512, st=2), w("fg", s.start, s.stop), w("dq", s.start, s.stop), A.add)
         pick(w("brow"), w("it"), w("offm"), "s")
+        for b in range(4):
+            pick(w("fg", 128 * b, 128 * b + 128), w("win%d" % b, 0, 256), w("offm"), "s", 0.5)
         a8 = w("tt", 0, 128, st=16)
         ts(w("fi"), a8, -7.5, 0.0625, A.add, A.mult)
         filler(2)
@@ -442,25 +459,22 @@ def rank_program(g, core, T, topo):
             same(c)
         filler()
         scan(w("sc"), w("ee"), w("kk"))
-        filler()
+        mean(0)
         tt(w("offi", 0, 4), w("p2", 0, 4), w("sc", 127, 512, st=128), A.max)
         tt(w("offi", 4, 8), w("p2", 4, 8), w("sc", 575, 768, st=64), A.max)
-        filler()
+        mean(1)
         scatter(w("inv"), w("offi"), w("sl"))
-        filler()
+        mean(2)
         turn(w("t512"), w("inv", 0, 512))
-        filler()
+        mean(3)
         tt(w("noff"), w("t512", 0, 512, st=32), w("t512", 16, 512, st=32), A.max)
         filler()
 
-    def renew(r):
-        for b in (2, 3):
-            pick(w("oth", 256 * b - 512, 256 * b - 256), w("win%d" % b), w("noff"), "s")
-        for b in (0, 1):
-            o, wn, nf, fw = w("nx", b, 1024, st=4), w("win%d" % b), w("noff"), w("fh", 256 * b, 256 * b + 256)
-            op("v", lambda: g.vector.tensor_tensor(o[0], wn[0].indirect(nf[0]), fw[0], A.add), [o], [wn, nf, fw])
-        for b in (2, 3):
-            tt(w("nx", b, 1024, st=4), w("oth", 256 * b - 512, 256 * b - 256), w("pa%d" % b, 0, 256), A.add)
+    def renew(r, fillers):
+        for b in range(4):
+            pick(w("nx", b, 1024, st=4), w("win%d" % b), w("noff"), "svsv"[b], 2.0)
+        if fillers:
+            fillers.pop(0)()
         quant("qx%d" % (r + 1), "nx", 0, 256)
 
     pieces = []
@@ -470,55 +484,61 @@ def rank_program(g, core, T, topo):
         for b in range(4):
             if r:
                 unpacked(b, "svsv"[b])
+        for b in range(4):
             pick(w("mt", b, 512, st=4), w("win%d" % b, 0, 256), w("offm"), "svsv"[b], 2.0)
+        if r:
+            pieces.pop(0)()
         quant("qm", "mt", c0)
         if r < 2:
             for nm in ("", "_s"):
                 send(donor, w("qm" + nm, c0, c0 + 128), w("qml" + nm, c0, c0 + 128), "am%d" % r)
             expect(asker, [w("qml", c0, c0 + 128), w("qml_s", c0, c0 + 128)], "am%d" % r)
             if r == 0:
-                candidates()
+                for b in range(4):
+                    lists("rte", 0, b, "ssss")
+                pieces = requests()
                 late_constants()
-            while pieces:
+                candidates()
+                mask1()
+            while r and pieces:
                 pieces.pop(0)()
             layer("qml", c0, "qh", c0, "qw")
             for nm in ("", "_s"):
                 send(asker, w("qh" + nm, c0, c0 + 128), w("qx%d" % r + nm, 256, 384), "ah%d" % r)
             expect(donor, [w("qx%d" % r, 256, 384), w("qx%d_s" % r, 256, 384)], "ah%d" % r)
-            if r == 0:
-                for b in range(4):
-                    lists("rte", 0, b, "ssss")
-                for piece in requests():
-                    piece()
-        else:
-            layer("qm", c0, "qx2", 256, "qwl")
             while pieces:
                 pieces.pop(0)()
+            if r == 0:
+                mask2()
+        else:
+            while pieces:
+                pieces.pop(0)()
+            layer("qm", c0, "qx2", 256, "qwl")
         copy(w("inv", 0, 512), w("cini"), "s")
         mm("pb0", 128, "qx%d" % r, 256, "qup")
         for b in range(4):
-            mm("pa%d" % b, 384, "qe", 128 * b, "qx%d" % r)
+            mm("pa%d" % b, 128, "qe", 128 * b, "qx%d" % r, 256)
         for b in range(4):
-            copy(w("win%d" % b, 256, 512, st=2), w("pa%d" % b, 256, 384), "s")
-            if b < 2:
-                copy(w("fh", 256 * b, 256 * b + 256), w("pa%d" % b, 0, 256), "s")
+            halve(w("dq", 128 * b, 128 * b + 128), w("pa%d" % b, 0, 128))
         repair()
         if r == 2:
             dma("y", T.fo[:], T.map[0:1, 0:2048], [w("map", 0, 2048)], ())
         hops(places=r < 2)
         pieces = requests() if r < 2 else []
         newest(pieces)
-        renew(r)
+        renew(r, pieces)
         if r < 2:
-            if pieces:
-                pieces.pop(0)()
             unpack(r + 1)
+            for _ in range(3):
+                pieces.pop(0)()
     dma("y", T.oc[:], T.qx3[:, 0:256].bitcast(dt.uint8), [w("qx3", 0, 256)], ())
     for k in range(4):
         dma("s", T.osc[4 * k:4 * k + 4, :], T.qx3_s[32 * k:32 * k + 4, 0:256], [w("qx3_s", 0, 256)], ())
-    mm("pb1", 256, "qv", 0, "qx3")
-    copy(w("yt"), w("pb1", 0, 256))
-    dma("y", T.y[:], T.yt[:], [w("yt")], ())
+    for b in range(2):
+        c = 128 * b
+        mm("pb%d" % (1 + b), 128, "qv", 0, "qx3", c)
+        copy(w("yt", c, c + 128), w("pb%d" % (1 + b), 0, 128), "vs"[b])
+        dma("ys"[b], T.y[:, c:c + 128], T.yt[:, c:c + 128], [w("yt", c, c + 128)], ())
     for sem, n in count.items():
         if known["g"].get(sem, 0) < n:
             g.wait_ge(T.sem[sem], n)

@@ -35,8 +35,8 @@ for _n, _k in [("mpa", 128), ("ari", 64), ("ci8", 8), ("fi", 8)]:
     _sb(_n, _k, "int32")
 for _n, _k in [("ra", 1024), ("it", 256), ("map", 2304), ("cw", 256), ("cwa", 256), ("cf", 32), ("gc", 144), ("grow", 32), ("dg", 16), ("rt", 128), ("tt", 128),
                ("rte", 128), ("tte", 128), ("cr", 128), ("ctr", 128), ("c32", 32), ("e8", 8), ("lw", 8), ("k1", 32), ("eq", 32), ("kb4", 132), ("kbs", 132),
-               ("ktri", 132), ("gi", 8), ("w8", 8), ("rr", 8), ("cu", 32), ("x64", 64), ("d32", 32), ("t1", 32), ("e32", 32),
-               ("m32", 32), ("l32", 32), ("t64", 64), ("p64", 64), ("row", 256), ("t2", 256), ("oof", 16), ("ulf", 8), ("tri", 32), ("i32", 32),
+               ("ktri", 132), ("gi", 8), ("w8", 8), ("rr", 8), ("cu", 32), ("x64", 64), ("d32", 32), ("t1", 64), ("e32", 64),
+               ("m32", 64), ("l32", 64), ("t64", 64), ("p64", 64), ("row", 128), ("rowv", 128), ("t2", 128), ("oof", 16), ("ulf", 8), ("tri", 64), ("i32", 32),
                ("ki", 768), ("dq", 512), ("fg", 512), ("v32", 32), ("h32", 32), ("gc0", 16), ("p1", 8), ("p2", 8), ("yt", 256)]:
     _sb(_n, _k)
 
@@ -232,9 +232,6 @@ def rank_program(g, core, T, topo):
     def late_iotas():
         iota(w("ki", 0, 512), [[-16, 4], [1, 128]], 0, 0)
         iota(w("ki", 512, 768), [[-16, 4], [1, 64]], 0, 0)
-        iota(w("ee"), [[0, 768]], 0, 0)
-        for b in range(4):
-            iota(w("win%d" % b, 256, 512), [[0, 256]], 0, 0)
 
     def bits(c, sh, m):
         o, i = w("ci8", c, c + 1), w("ci8", 0, 1)
@@ -257,26 +254,28 @@ def rank_program(g, core, T, topo):
     ts(w("dg"), w("i32", 0, 16), QQ, None, A.is_equal)
     ts(H16, HH, 16.0, None, A.mult)
     ts(w("gc", 0, 16), w("gc0"), QQ, None, A.add)
-    ts(w("tri"), w("i32"), II, None, A.is_gt)
+    ts(w("tri", 0, 32), w("i32"), II, None, A.is_gt)
+    fill(w("tri", 32, 64), 1.0)
+    for a in (32, 96):
+        fill(w("e32", 32, 64, a, a + 32), -1.0)
     ts(TJ, PP, 2048.0, None, A.add)
     for k in range(4):
         ts(MK[k], KR, float(k), None, A.is_equal)
     ts(TJC, TJ, ROUND, None, A.add)
     ts(NQ, QQ, -1.0, -0.5, A.mult, A.add)
     ts(cf(10), QQ, 4.0, None, A.mult)
-    ts(w("oof", 0, 1), QQ, H16, None, A.add)
-    ts(cf(11), QQ, 16.0, None, A.add)
-    tt(w("oof", 1, 2), cf(11), H16, A.subtract)
-    ts(w("oof", 2, 4), w("oof", 0, 2), 32.0, None, A.add)
-    copy(w("oo", 0, 4), w("oof", 0, 4))
 
     def late_constants():
+        ts(w("oof", 0, 1), QQ, H16, None, A.add)
+        ts(cf(11), QQ, 16.0, None, A.add)
         fill(w("ulf"), 0.0)
         ts(w("ktri"), w("ktri"), 3.0, None, A.is_lt)
+        tt(w("oof", 1, 2), cf(11), H16, A.subtract)
         ts(w("gi"), w("gi"), 256.0 * UNIT, None, A.mult)
         for c in range(4):
             ts(w("ulf", c, c + 1), Q2, 16.0, float(c // 2), A.mult, A.add)
         fill(w("kb4"), 0.0)
+        copy(w("oo", 0, 2), w("oof", 0, 2))
         copy(w("ul"), w("ulf"))
         ts(w("w8"), w("w8"), cf(10), None, A.add)
         ts(w("h32"), w("h32"), HH, None, A.is_equal)
@@ -309,15 +308,17 @@ def rank_program(g, core, T, topo):
         tt(w("cw"), w("cw"), w("cwa"), A.add)
 
     def mapw(m):
-        return w("map", 256 * m, 256 * m + 256)
+        return w("map", 256 * m, 256 * m + 256 if m else 128)
     for a in range(4):
         copy(w("offa", 0, 32, 32 * a, 32 * a + 32), w("mpa", 0, 32, 0, 32))
     for m in range(8):
         if m == 1:
             for a in range(4):
                 copy(w("offa", 32, 128, 32 * a, 32 * a + 32), w("mpa", 32, 128, 0, 32))
-        if m not in (3, 6):
-            pick(mapw(m), w("it"), w("offa", 16 * m, 16 * m + 16), "v" if m == 0 else "s")
+        if m == 0:
+            pick(w("map", 0, 128), w("it"), w("offa", 0, 8))
+        elif m not in (3, 6):
+            pick(mapw(m), w("it"), w("offa", 16 * m, 16 * m + 16), "s")
 
     def step1(m):
         gr, mp, of, dg = w("grow", 16 * (m % 2), 16 * (m % 2) + 16), mapw(m), w("off", 2 * m, 2 * m + 1), w("dg")
@@ -327,10 +328,10 @@ def rank_program(g, core, T, topo):
         o, i = w("off", 2 * m + 2, 2 * m + 3), w("grow", 16 * (m % 2), 16 * (m % 2) + 16)
         op("v", lambda: g.vector.tensor_reduce(o[0], i[0], AxisListType.X, A.max), [o], [i])
 
-    def hop(m, extra):
+    def hop(m, extra, known0):
         gc = w("gc", 16 * m + 16, 16 * m + 32)
         pick(gc, mapw(m), w("off", 2 * m, 2 * m + 1), "v" if m == 7 else "s")
-        if m < 7:
+        if m < 7 and not (known0 and m == 0):
             step1(m)
             if extra:
                 extra.pop(0)()
@@ -342,9 +343,9 @@ def rank_program(g, core, T, topo):
         for a in range(4):
             copy(w(buf, 32 * a, 32 * a + 32, 32 * b, 32 * b + 32), w("gc", c0 + 32 * b, c0 + 32 * b + 32, 32 * a, 32 * a + 32), qs[a])
 
-    def hops(extra=None, places=False):
+    def hops(extra=None, places=False, known0=True):
         for m in range(8):
-            hop(m, extra)
+            hop(m, extra, known0)
             if m % 2:
                 lists("rt", 16, m // 2, "ssss" if m < 7 else "vsvs")
             if places and m in (0, 2, 4, 7):
@@ -363,7 +364,7 @@ def rank_program(g, core, T, topo):
         quant("qe", "zt", 128 * b, 128, 3 - b)
     hops([lambda: constant(0), lambda: pick(mapw(3), w("it"), w("offa", 48, 64)), lambda: constant(1), lambda: constant(2), lambda: constant(3),
           lambda: quant("qx0", "xt", 0, 256), lambda: (unpack(0), pick(mapw(6), w("it"), w("offa", 96, 112))), lambda: copy(w("aro"), w("ari")),
-          lambda: None, lambda: unpacked(0, "v"), lambda: unpacked(1, "v"), lambda: unpacked(2, "v"), lambda: unpacked(3, "v")])
+          lambda: None, lambda: unpacked(0, "v"), lambda: unpacked(1, "v"), lambda: unpacked(2, "v"), lambda: unpacked(3, "v")], known0=False)
     far = (rank + 4) % N
     for nm in ("", "_s"):
         send(far, w("qw" + nm), w("qwl" + nm), "aw")
@@ -385,9 +386,9 @@ def rank_program(g, core, T, topo):
         return [lambda: step1(7), lambda: turn(w("tte"), w("rte")), lambda: step2(7), lambda: copy(w("offe"), w("tte", 0, 128, st=16)),
                 lambda: pick(w("cr"), w("cw"), w("offe")),
                 lambda: (ts(w("e8"), w("off", 0, 16, st=2), UNIT, None, A.mult), turn(w("ctr"), w("cr")), copy(w("lw"), w("off", 2, 18, st=2))),
-                lambda: (tt(w("e8"), w("e8"), w("gi"), A.add), cells(0), cells(1)), lambda: (cells(2), cells(3)),
-                lambda: (sums(0), sums(1)), lambda: (sums(2), sums(3)),
-                lambda: ts(w("eq"), w("eq"), P21, None, A.mult),
+                lambda: (tt(w("e8"), w("e8"), w("gi"), A.add), cells(0)), lambda: (cells(1), cells(2), cells(3)),
+                lambda: (sums(0), sums(1)), lambda: sums(2),
+                lambda: (sums(3), ts(w("eq"), w("eq"), P21, None, A.mult)),
                 lambda: (keys(0), keys(1), keys(2), keys(3))]
 
     def layer(src, c0, dst, d0, lay, qs="svsv"):
@@ -407,30 +408,38 @@ def rank_program(g, core, T, topo):
         ts(w("kb4", 2, 128, st=8), w("pb0", 32, 64, st=2), 0.0, P21, A.is_gt, A.mult)
         ts(w("kb4", 6, 128, st=8), w("pb0", 33, 64, st=2), 0.0, P21, A.is_le, A.mult)
         scan(w("kbs"), w("kb4"), w("ktri"))
-        R, V1, VF, EF, LO = w("rr", 0, 1), w("rr", 1, 2), w("rr", 2, 3), w("e32", 0, 1), w("l32", 31, 32)
+        R, V1, VF, F0, DV = [w("rr", c, c + 1) for c in range(5)]
+        EF, LO = w("e32", 0, 1), w("l32", 63, 64)
         o, i = R, w("kbs", 2, 132, st=4)
         op("v", lambda: g.vector.tensor_reduce(o[0], i[0], AxisListType.X, A.min), [o], [i])
-        ts(w("e32"), w("cu"), R, ROUND, A.mult, A.add)
+        ts(w("e32", 0, 32), w("cu"), R, ROUND, A.mult, A.add)
+        for a in (0, 64):
+            ts(w("e32", 32, 64, a, a + 32), w("cu", 0, 32, a + 32, a + 64), w("rr", 0, 1, a + 32, a + 64), ROUND, A.mult, A.add)
         turn(w("t1"), w("e32"))
         ts(V1, EF, -ROUND, -UNIT, A.add, A.mult)
+        ts(F0, R, 256.0 * UNIT, None, A.is_lt)
         ts(w("m32"), w("t1"), EF, None, A.is_equal)
         tt(VF, V1, R, A.add)
-        ts(w("d32"), w("e32"), -1.0, TJC, A.mult, A.add)
+        ts(w("d32"), w("e32", 0, 32), -1.0, TJC, A.mult, A.add)
         scan(w("l32"), w("m32"), w("tri"))
         ts(w("x64", 32, 64), w("cu"), UNIT, VF, A.mult, A.mult)
+        tt(DV, VF, w("lw", 0, 1), A.subtract)
         ts(w("x64", 0, 32), w("d32"), LO, EF, A.mult, A.add)
+        ts(w("off", 2, 3), DV, F0, w("lw", 0, 1), A.mult, A.add)
         turn(w("t64"), w("x64"))
-        pick(w("p64"), w("t64"), w("oo", 0, 4))
-        for i in range(8):
-            a, b = 2 * (i // 4) + i % 2, 2 * (i // 4) + i // 2 % 2
-            copy(w("row", 64 * a, 64 * a + 64, 32 * b, 32 * b + 32), w("p64", 0, 64, 32 * a, 32 * a + 32), "vsvvsvsv"[i])
-        copy(w("row", 0, 128, 64, 128), w("row", 0, 128, 0, 64), "v")
-        copy(w("row", 128, 256, 0, 64), w("row", 128, 256, 64, 128), "s")
+        pick(w("p64", 0, 32), w("t64", 0, 32), w("oo", 0, 2))
+        pick(w("p64", 32, 64), w("t64", 32, 64), w("oo", 0, 2), "s")
+        for c, qs in ((0, "vsvvsvvv"), (32, "ssssssss")):
+            buf = "rowv" if c else "row"
+            for i in range(8):
+                a, b = 2 * (i // 4) + i % 2, 2 * (i // 4) + i // 2 % 2
+                copy(w(buf, 32 * a, 32 * a + 32, 32 * b, 32 * b + 32), w("p64", c, c + 32, 32 * a, 32 * a + 32), qs[i])
+            copy(w(buf, 0, 64, 64, 128), w(buf, 0, 64, 0, 64), qs[7])
+            copy(w(buf, 64, 128, 0, 64), w(buf, 64, 128, 64, 128), qs[7])
         turn(w("t2"), w("row"))
-        for s in range(2):
-            ts(w("offr", s, 8, st=2), w("t2", 16 * s, 256, st=64), -ROUND, None, A.add)
-        for b in range(4):
-            scatter(w("map"), w("offr", 2 * b, 2 * b + 2), w("row", 64 * b + 32, 64 * b + 64))
+        ts(w("offr"), w("t2", 0, 128, st=16), -ROUND, None, A.add)
+        for b in range(2):
+            scatter(w("map"), w("offr", 4 * b, 4 * b + 4), w("rowv", 64 * b, 64 * b + 64))
 
     def newest(fillers):
         def filler(n=1):
@@ -498,6 +507,7 @@ def rank_program(g, core, T, topo):
                     lists("rte", 0, b, "ssss")
                 pieces = requests()
                 late_constants()
+                pick(w("map", 128, 256), w("it"), w("offa", 8, 16), "s")
                 candidates()
                 mask1()
             while r and pieces:
@@ -506,20 +516,26 @@ def rank_program(g, core, T, topo):
             for nm in ("", "_s"):
                 send(asker, w("qh" + nm, c0, c0 + 128), w("qx%d" % r + nm, 256, 384), "ah%d" % r)
             expect(donor, [w("qx%d" % r, 256, 384), w("qx%d_s" % r, 256, 384)], "ah%d" % r)
+            if r == 0:
+                iota(w("ee"), [[0, 768]], 0, 0)
             while pieces:
                 pieces.pop(0)()
             if r == 0:
                 mask2()
         else:
-            while pieces:
+            while len(pieces) > 1:
                 pieces.pop(0)()
             layer("qm", c0, "qx2", 256, "qwl")
+            pieces.pop(0)()
         copy(w("inv", 0, 512), w("cini"), "s")
         mm("pb0", 128, "qx%d" % r, 256, "qup")
         for b in range(4):
             mm("pa%d" % b, 128, "qe", 128 * b, "qx%d" % r, 256)
         for b in range(4):
             halve(w("dq", 128 * b, 128 * b + 128), w("pa%d" % b, 0, 128))
+        if r == 0:
+            for b in range(4):
+                copy(w("win%d" % b, 256, 512), w("ee", 0, 256), "s")
         repair()
         if r == 2:
             dma("y", T.fo[:], T.map[0:1, 0:2048], [w("map", 0, 2048)], ())
@@ -529,7 +545,7 @@ def rank_program(g, core, T, topo):
         renew(r, pieces)
         if r < 2:
             unpack(r + 1)
-            for _ in range(3):
+            for _ in range(2):
                 pieces.pop(0)()
     dma("y", T.oc[:], T.qx3[:, 0:256].bitcast(dt.uint8), [w("qx3", 0, 256)], ())
     for k in range(4):

import math
from concourse.mybir import dt, AluOpType as A, AxisListType, ActivationFunctionType as F

N = 8
STEP = [1, 2, 4]
UNIT = 512.0
P21 = 2097152.0
ROUND = 12582912.0
SCRATCH = {}
SEMAPHORES = ["cv", "cs", "ct", "cg", "am0", "am1", "ah0", "ah1", "aw"] + ["d%d" % i for i in range(24)] + ["l%d" % i for i in range(16)]


def _sb(name, n, dtype="float32"):
    SCRATCH[name] = ("sbuf", [128, n], dtype)


def _mx(name, n):
    _sb(name, n, "float8_e4m3fn_x4")
    _sb(name + "_s", n, "uint8")


for _b in range(4):
    SCRATCH["pa%d" % _b] = ("psum", [128, 512], "float32")
    SCRATCH["pb%d" % _b] = ("psum", [128, 512], "float32")
    _sb("win%d" % _b, 512, "bfloat16")
    _mx("qx%d" % _b, 384)
for _n, _k in [("qe", 512), ("qm", 384), ("qml", 256), ("qh", 256), ("qw", 512), ("qwl", 512), ("qu", 128), ("qup", 128), ("qv", 128)]:
    _mx(_n, _k)
for _n, _k in [("xt", 1024), ("ut", 512), ("vt", 512), ("mt", 512), ("ht", 512), ("nx", 1024), ("zt", 528), ("zs", 528),
               ("cini", 512), ("itz", 256), ("sl", 128), ("inv", 1024), ("t512", 512), ("kk", 768), ("ee", 768), ("sc", 768), ("brow", 128)]:
    _sb(_n, _k, "bfloat16")
for _n, _k in [("offa", 128), ("aro", 64), ("off", 18), ("offm", 8), ("offe", 8), ("offr", 8), ("oo", 8), ("ul", 8), ("offi", 8), ("noff", 16), ("cil", 32)]:
    _sb(_n, _k, "uint16")
for _n, _k in [("mpa", 128), ("ari", 64), ("ci8", 8), ("fi", 8)]:
    _sb(_n, _k, "int32")
for _n, _k in [("ra", 1024), ("it", 256), ("map", 2304), ("cw", 256), ("cwa", 256), ("cf", 32), ("gc", 144), ("grow", 32), ("dg", 16), ("rt", 128), ("tt", 128),
               ("rte", 128), ("tte", 128), ("cr", 128), ("ctr", 128), ("c32", 32), ("e8", 8), ("lw", 8), ("k1", 32), ("eq", 32), ("kb4", 132), ("kbs", 132),
               ("ktri", 132), ("gi", 8), ("w8", 8), ("rr", 8), ("cu", 32), ("x64", 64), ("d32", 32), ("t1", 64), ("e32", 64),
               ("m32", 64), ("l32", 64), ("t64", 64), ("p64", 64), ("row", 128), ("rowv", 128), ("t2", 128), ("oof", 16), ("ulf", 8), ("tri", 64), ("i32", 32),
               ("ki", 768), ("dq", 512), ("fg", 512), ("v32", 32), ("h32", 32), ("gc0", 16), ("p1", 8), ("p2", 8), ("yt", 256)]:
    _sb(_n, _k)

CODES = {n for n, s in SCRATCH.items() if s[2] == "float8_e4m3fn_x4"}
PSUM = {n for n, s in SCRATCH.items() if s[0] == "psum"}


def rank_program(g, core, T, topo):
    rank = T.rank_of(core)
    if rank is None:
        return
    Q = {"g": g, "v": g.vector, "s": g.scalar, "t": g.tensor, "y": g.sync}
    known = {q: {} for q in Q}
    hist = {}
    count = {}
    nd = [1]
    nl = [0]

    def w(name, c0=0, c1=None, p0=0, p1=128, st=1):
        t = T[name]
        if c1 is None:
            c1 = t.shape[1]
        if p0 == 0 and p1 == 128:
            ap = t[:, c0:c1] if st == 1 else t[:, c0:c1:st]
        else:
            ap = t[p0:p1, c0:c1] if st == 1 else t[p0:p1, c0:c1:st]
        return (ap, name, p0, p1, c0, c1, st)

    def overlap(a, b):
        if a[2] >= b[3] or b[2] >= a[3] or a[4] >= b[5] or b[4] >= a[5]:
            return False
        return (a[4] - b[4]) % math.gcd(a[6], b[6]) == 0

    def covers(a, b):
        return a[2] <= b[2] and a[3] >= b[3] and a[4] <= b[4] and a[5] >= b[5] and (a[6] == 1 or (a[6] == b[6] and (a[4] - b[4]) % a[6] == 0))

    def order(q, reads, writes, compute):
        need = []
        for isw, vs in ((False, reads), (True, writes)):
            for x in vs:
                for (y, yw, yq, sem, val, clock, ycomp) in hist.get(x[1], []):
                    same = yq == q and compute and ycomp
                    if same and not yw:
                        continue
                    if x[1] not in PSUM and (not overlap(x, y) or not (isw or yw)):
                        continue
                    need.append((sem, val, clock))
        for sem, val, clock in reversed(need):
            if known[q].get(sem, 0) >= val:
                continue
            Q[q].wait_ge(T.sem[sem], val)
            for k, n in clock.items():
                if known[q].get(k, 0) < n:
                    known[q][k] = n
            known[q][sem] = val

    def note(q, reads, writes, sem, val, compute):
        clock = dict(known.get(q, {}))
        for isw, vs in ((False, reads), (True, writes)):
            for x in vs:
                h = hist.setdefault(x[1], [])
                if isw:
                    h[:] = [r for r in h if not covers(x, r[0])]
                h.append((x, isw, q, sem, val, clock, compute))

    def op(q, call, writes, reads):
        order(q, reads, writes, True)
        sem = "c" + q
        count[sem] = count.get(sem, 0) + 1
        call().then_inc(T.sem[sem], 1)
        note(q, reads, writes, sem, count[sem], True)

    def dma(q, out, in_, reads=(), writes=(), group=None):
        order(q, reads, writes, False)
        if group is None:
            sem = "d%d" % nd[0]
            nd[0] += 1
            total = 16
        else:
            sem, total = group
        count[sem] = total
        Q[q].dma_start(out, in_).then_inc(T.sem[sem], 16)
        note(q, reads, writes, sem, total, False)

    def raw(x):
        return x[0].bitcast(dt.uint8) if x[1] in CODES else x[0]

    def send(to, src, dst, sem):
        dc = T.cores[to]
        order("g", [src], [], False)
        rid, pid, _ = topo.addr(dc)
        l = "l%d" % nl[0]
        nl[0] += 1
        g.remote_dma(raw(dst), raw(src), T.sem[sem], T.sem[l], pid, rid, sum(1 << e for e in engines(rank)))
        count[l] = len(engines(rank))
        note("g", [src], [], l, count[l], False)

    def engines(r):
        return topo.engines(T.cores[r], T.cores[(r + 4) % N])

    def expect(frm, views, sem):
        n = len(engines(frm)) * len(views)
        count[sem] = n
        note("x", [], views, sem, n, False)

    def copy(out, in_, q="v"):
        if q == "v":
            op("v", lambda: g.vector.tensor_copy(out[0], in_[0]), [out], [in_])
        else:
            op("s", lambda: g.scalar.activation(out[0], in_[0], F.Copy), [out], [in_])

    def pick(out, win, off, q="v", scale=None):
        rd = [win, off]
        if q == "v":
            if scale is None:
                op("v", lambda: g.vector.tensor_copy(out[0], win[0].indirect(off[0])), [out], rd)
            else:
                op("v", lambda: g.vector.tensor_scalar(out[0], win[0].indirect(off[0]), scale, None, A.mult), [out], rd)
        elif scale is None:
            op("s", lambda: g.scalar.activation(out[0], win[0].indirect(off[0]), F.Copy), [out], rd)
        elif isinstance(scale, float):
            op("s", lambda: g.scalar.activation(out[0], win[0].indirect(off[0]), F.Copy, scale=scale), [out], rd)
        else:
            op("s", lambda: g.scalar.activation(out[0], win[0].indirect(off[0]), F.Copy, scale=scale[0]), [out], rd + [scale])

    def halve(out, in_):
        op("s", lambda: g.scalar.activation(out[0], in_[0], F.Copy, scale=0.5), [out], [in_])

    def scatter(win, off, in_):
        op("v", lambda: g.vector.tensor_copy(win[0].indirect(off[0]), in_[0]), [win], [off, in_])

    def tt(out, a, b, o):
        op("v", lambda: g.vector.tensor_tensor(out[0], a[0], b[0], o), [out], [a, b])

    def ts(out, a, s1, s2, o1, o2=None):
        rd = [a] + [s for s in (s1, s2) if isinstance(s, tuple)]
        x1 = s1[0] if isinstance(s1, tuple) else s1
        x2 = s2[0] if isinstance(s2, tuple) else s2
        if o2 is None:
            op("v", lambda: g.vector.tensor_scalar(out[0], a[0], x1, None, o1), [out], rd)
        else:
            op("v", lambda: g.vector.tensor_scalar(out[0], a[0], x1, x2, o1, o2), [out], rd)

    def scan(out, d0, d1):
        op("v", lambda: g.vector.tensor_tensor_scan(out[0], d0[0], d1[0], 0.0, A.max, A.mult), [out], [d0, d1])

    def turn(out, a):
        op("v", lambda: g.vector.transpose(out[0], a[0]), [out], [a])

    def fill(out, c):
        op("v", lambda: g.vector.memset(out[0], c), [out], [])

    def iota(out, pattern, base, cm):
        op("g", lambda: g.iota(out[0], pattern, base, cm, allow_small_or_imprecise_dtypes=True), [out], [])

    def quant(name, tile, c0=0, n=128, t0=0):
        o, s, i = w(name, c0, c0 + n), w(name + "_s", c0, c0 + n), w(tile, t0, t0 + 4 * n)
        op("v", lambda: g.vector.quantize_mx(o[0], s[0], i[0]), [o, s], [i])

    def mm(ps, n, l, lc, r, rc=0):
        o = w(ps, 0, n)
        a, b, c, d = w(l, lc, lc + 128), w(l + "_s", lc, lc + 128), w(r, rc, rc + n), w(r + "_s", rc, rc + n)
        op("t", lambda: g.tensor.matmul_mx(o[0], a[0], b[0], c[0], d[0], True, True), [o], [a, b, c, d])

    for q, h in (("y", 0), ("s", 1)):
        for m in range(8):
            dma(q, T.mpa[16 * h:16 * h + 16, 16 * m:16 * m + 16], T.mp[16 * m:16 * m + 16, :], (), [w("mpa", 16 * m, 16 * m + 16, 16 * h, 16 * h + 16)], ("d0", 256))
        if h == 0:
            dma("y", T.xt[:], T.x[:], (), [w("xt")])
    dma("s", T.ari[:], T.ar[:], (), [w("ari")])
    dma("y", T.qw[:].bitcast(dt.uint8), T.wc[:], (), [w("qw")])
    dma("y", T.qw_s[:], T.ws[:], (), [w("qw_s")])
    dma("s", T.ut[:], T.u[:], (), [w("ut")])
    dma("s", T.vt[:], T.v[:], (), [w("vt")])

    iota(w("ci8", 0, 1), [[1, 1]], 0, 1)
    iota(w("gc0"), [[-1, 16]], 127, -1)
    iota(w("it"), [[1, 256]], 0, 0)
    iota(w("i32"), [[1, 32]], 0, 0)
    fill(w("zs"), 0.5)
    fill(w("cu"), 1.0 / UNIT)
    z = w("zt", 0, 516)
    zs = w("zs", 0, 516)
    op("g", lambda: g.affine_select(z[0], zs[0], [[-1, 516]], A.is_equal, 0.0, 3, 4), [z], [zs])
    iota(w("gi"), [[1, 8]], 0, 0)
    iota(w("w8"), [[64, 8]], 512, 0)
    iota(w("ktri"), [[0, 33], [1, 4]], 0, 0)
    iota(w("v32"), [[16, 16], [0, 2]], 0, 0)
    iota(w("h32"), [[0, 16], [1, 2]], 0, 0)
    iota(w("sl"), [[2, 128]], 256, 0)
    iota(w("itz"), [[1, 256]], 0, 0)

    def late_iotas():
        iota(w("ki", 0, 512), [[-16, 4], [1, 128]], 0, 0)
        iota(w("ki", 512, 768), [[-16, 4], [1, 64]], 0, 0)

    def bits(c, sh, m):
        o, i = w("ci8", c, c + 1), w("ci8", 0, 1)
        if sh:
            op("v", lambda: g.vector.tensor_scalar(o[0], i[0], sh, m, A.arith_shift_right, A.bitwise_and), [o], [i])
        else:
            op("v", lambda: g.vector.tensor_scalar(o[0], i[0], m, None, A.bitwise_and), [o], [i])
    bits(1, 0, 15)
    bits(2, 4, 1)
    bits(3, 0, 31)
    bits(4, 2, 3)
    bits(5, 1, 7)
    copy(w("cf", 0, 6), w("ci8", 0, 6))

    def cf(c):
        return w("cf", c, c + 1)
    PP, QQ, HH, II, KR, Q2, H16, TJ, TJC, NQ = [cf(c) for c in range(10)]
    MK = [cf(12 + k) for k in range(4)]
    ts(w("off", 0, 1), PP, -1.0, 127.0, A.mult, A.add)
    ts(w("dg"), w("i32", 0, 16), QQ, None, A.is_equal)
    ts(H16, HH, 16.0, None, A.mult)
    ts(w("gc", 0, 16), w("gc0"), QQ, None, A.add)
    ts(w("tri", 0, 32), w("i32"), II, None, A.is_gt)
    fill(w("tri", 32, 64), 1.0)
    for a in (32, 96):
        fill(w("e32", 32, 64, a, a + 32), -1.0)
    ts(TJ, PP, 2048.0, None, A.add)
    for k in range(4):
        ts(MK[k], KR, float(k), None, A.is_equal)
    ts(TJC, TJ, ROUND, None, A.add)
    ts(NQ, QQ, -1.0, -0.5, A.mult, A.add)
    ts(cf(10), QQ, 4.0, None, A.mult)

    def late_constants():
        ts(w("oof", 0, 1), QQ, H16, None, A.add)
        ts(cf(11), QQ, 16.0, None, A.add)
        fill(w("ulf"), 0.0)
        ts(w("ktri"), w("ktri"), 3.0, None, A.is_lt)
        tt(w("oof", 1, 2), cf(11), H16, A.subtract)
        ts(w("gi"), w("gi"), 256.0 * UNIT, None, A.mult)
        for c in range(4):
            ts(w("ulf", c, c + 1), Q2, 16.0, float(c // 2), A.mult, A.add)
        fill(w("kb4"), 0.0)
        copy(w("oo", 0, 2), w("oof", 0, 2))
        copy(w("ul"), w("ulf"))
        ts(w("w8"), w("w8"), cf(10), None, A.add)
        ts(w("h32"), w("h32"), HH, None, A.is_equal)
        ts(w("v32"), w("v32"), QQ, None, A.add)
        quant("qu", "ut")
        tt(w("v32"), w("v32"), w("h32"), A.mult)
        quant("qv", "vt")
        copy(w("cil"), w("v32"))
        ts(w("kb4", 128, 129), TJ, UNIT, None, A.mult)
        o4, i4, l = w("qup"), w("qu"), w("ul")
        op("v", lambda: g.vector.tensor_copy(o4[0].bitcast(dt.uint32), i4[0].bitcast(dt.uint32).indirect(l[0])), [o4], [i4, l])
        o2, i2 = w("qup_s"), w("qu_s")
        op("v", lambda: g.vector.tensor_copy(o2[0], i2[0].indirect(l[0])), [o2], [i2, l])

    def mask1():
        o, i, n, o3 = w("ki"), w("ki"), NQ, w("kk")
        op("s", lambda: g.scalar.activation(o[0], i[0], F.Sign, bias=n[0]), [o], [i, n])
        op("s", lambda: g.scalar.activation(o3[0], i[0], F.Relu), [o3], [i])

    def mask2():
        tt(w("kk", 127, 512, st=128), w("kk", 127, 512, st=128), w("w8", 0, 4), A.mult)
        tt(w("kk", 575, 768, st=64), w("kk", 575, 768, st=64), w("w8", 4, 8), A.mult)
        pick(w("cini"), w("itz"), w("cil"), "s")

    def candidates():
        for k in range(4):
            pick(w("ra", 256 * k, 256 * k + 256), w("it"), w("aro", 16 * k, 16 * k + 16), "s", MK[k])
        tt(w("cw"), w("ra", 0, 256), w("ra", 256, 512), A.add)
        tt(w("cwa"), w("ra", 512, 768), w("ra", 768, 1024), A.add)
        tt(w("cw"), w("cw"), w("cwa"), A.add)

    def mapw(m):
        return w("map", 256 * m, 256 * m + 256 if m else 128)
    for a in range(4):
        copy(w("offa", 0, 32, 32 * a, 32 * a + 32), w("mpa", 0, 32, 0, 32))
    for m in range(8):
        if m == 1:
            for a in range(4):
                copy(w("offa", 32, 128, 32 * a, 32 * a + 32), w("mpa", 32, 128, 0, 32))
        if m == 0:
            pick(w("map", 0, 128), w("it"), w("offa", 0, 8))
        elif m not in (3, 6):
            pick(mapw(m), w("it"), w("offa", 16 * m, 16 * m + 16), "s")

    def step1(m):
        gr, mp, of, dg = w("grow", 16 * (m % 2), 16 * (m % 2) + 16), mapw(m), w("off", 2 * m, 2 * m + 1), w("dg")
        op("v", lambda: g.vector.tensor_tensor(gr[0], mp[0].indirect(of[0]), dg[0], A.mult), [gr], [mp, of, dg])

    def step2(m):
        o, i = w("off", 2 * m + 2, 2 * m + 3), w("grow", 16 * (m % 2), 16 * (m % 2) + 16)
        op("v", lambda: g.vector.tensor_reduce(o[0], i[0], AxisListType.X, A.max), [o], [i])

    def hop(m, extra, known0):
        gc = w("gc", 16 * m + 16, 16 * m + 32)
        pick(gc, mapw(m), w("off", 2 * m, 2 * m + 1), "v" if m == 7 else "s")
        if m < 7 and not (known0 and m == 0):
            step1(m)
            if extra:
                extra.pop(0)()
            step2(m)
        if extra:
            extra.pop(0)()

    def lists(buf, c0, b, qs):
        for a in range(4):
            copy(w(buf, 32 * a, 32 * a + 32, 32 * b, 32 * b + 32), w("gc", c0 + 32 * b, c0 + 32 * b + 32, 32 * a, 32 * a + 32), qs[a])

    def hops(extra=None, places=False, known0=True):
        for m in range(8):
            hop(m, extra, known0)
            if m % 2:
                lists("rt", 16, m // 2, "ssss" if m < 7 else "vsvs")
            if places and m in (0, 2, 4, 7):
                lists("rte", 0, (m + 1) // 2 - m // 7, "ssss")
        turn(w("tt"), w("rt"))
        copy(w("offm"), w("tt", 0, 128, st=16))

    def unpack(r):
        for b in range(4):
            mm("pa%d" % b, 256, "qe", 128 * b, "qx%d" % r)

    def unpacked(b, q):
        copy(w("win%d" % b, 0, 256), w("pa%d" % b, 0, 256), q)

    def constant(b):
        quant("qe", "zt", 128 * b, 128, 3 - b)
    hops([lambda: constant(0), lambda: pick(mapw(3), w("it"), w("offa", 48, 64)), lambda: constant(1), lambda: constant(2), lambda: constant(3),
          lambda: quant("qx0", "xt", 0, 256), lambda: (unpack(0), pick(mapw(6), w("it"), w("offa", 96, 112))), lambda: copy(w("aro"), w("ari")),
          lambda: None, lambda: unpacked(0, "v"), lambda: unpacked(1, "v"), lambda: unpacked(2, "v"), lambda: unpacked(3, "v")], known0=False)
    far = (rank + 4) % N
    for nm in ("", "_s"):
        send(far, w("qw" + nm), w("qwl" + nm), "aw")
    expect(far, [w("qwl"), w("qwl_s")], "aw")
    late_iotas()

    def requests():
        def cells(a):
            for b in range(4):
                copy(w("c32", 8 * a, 8 * a + 8, 32 * b, 32 * b + 32), w("ctr", 32 * b, 32 * b + 32, 32 * a, 32 * a + 32, st=4), "vsvs"[b])

        def sums(k):
            tt(w("k1", k, 32, st=4), w("c32", k, 32, st=4), w("e8"), A.add)
            tt(w("eq", k, 32, st=4), w("c32", k, 32, st=4), w("lw"), A.is_equal)

        def keys(k):
            s = 4 * (16 * (k // 2) + k % 2)
            tt(w("kb4", s, s + 64, st=8), w("k1", k, 32, st=4), w("eq", k, 32, st=4), A.max)
        return [lambda: step1(7), lambda: turn(w("tte"), w("rte")), lambda: step2(7), lambda: copy(w("offe"), w("tte", 0, 128, st=16)),
                lambda: pick(w("cr"), w("cw"), w("offe")),
                lambda: (ts(w("e8"), w("off", 0, 16, st=2), UNIT, None, A.mult), turn(w("ctr"), w("cr")), copy(w("lw"), w("off", 2, 18, st=2))),
                lambda: (tt(w("e8"), w("e8"), w("gi"), A.add), cells(0)), lambda: (cells(1), cells(2), cells(3)),
                lambda: (sums(0), sums(1)), lambda: sums(2),
                lambda: (sums(3), ts(w("eq"), w("eq"), P21, None, A.mult)),
                lambda: (keys(0), keys(1), keys(2), keys(3))]

    def layer(src, c0, dst, d0, lay, qs="svsv"):
        for b in range(4):
            mm("pb%d" % b, 128, lay, 128 * b, src, c0)
        for b in range(4):
            o, i = w("ht", b, 512, st=4), w("pb%d" % b, 0, 128)
            if qs[b] == "s":
                op("s", lambda: g.scalar.activation(o[0], i[0], F.Relu, scale=0.03125), [o], [i])
            else:
                ts(o, i, 0.0, 0.03125, A.max, A.mult)
        quant(dst, "ht", d0)

    def repair():
        ts(w("kb4", 1, 64, st=4), w("pb0", 0, 16), 0.0, P21, A.is_gt, A.mult)
        ts(w("kb4", 65, 128, st=4), w("pb0", 16, 32), 0.0, P21, A.is_le, A.mult)
        ts(w("kb4", 2, 128, st=8), w("pb0", 32, 64, st=2), 0.0, P21, A.is_gt, A.mult)
        ts(w("kb4", 6, 128, st=8), w("pb0", 33, 64, st=2), 0.0, P21, A.is_le, A.mult)
        scan(w("kbs"), w("kb4"), w("ktri"))
        R, V1, VF, F0, DV = [w("rr", c, c + 1) for c in range(5)]
        EF, LO = w("e32", 0, 1), w("l32", 63, 64)
        o, i = R, w("kbs", 2, 132, st=4)
        op("v", lambda: g.vector.tensor_reduce(o[0], i[0], AxisListType.X, A.min), [o], [i])
        ts(w("e32", 0, 32), w("cu"), R, ROUND, A.mult, A.add)
        for a in (0, 64):
            ts(w("e32", 32, 64, a, a + 32), w("cu", 0, 32, a + 32, a + 64), w("rr", 0, 1, a + 32, a + 64), ROUND, A.mult, A.add)
        turn(w("t1"), w("e32"))
        ts(V1, EF, -ROUND, -UNIT, A.add, A.mult)
        ts(F0, R, 256.0 * UNIT, None, A.is_lt)
        ts(w("m32"), w("t1"), EF, None, A.is_equal)
        tt(VF, V1, R, A.add)
        ts(w("d32"), w("e32", 0, 32), -1.0, TJC, A.mult, A.add)
        scan(w("l32"), w("m32"), w("tri"))
        ts(w("x64", 32, 64), w("cu"), UNIT, VF, A.mult, A.mult)
        tt(DV, VF, w("lw", 0, 1), A.subtract)
        ts(w("x64", 0, 32), w("d32"), LO, EF, A.mult, A.add)
        ts(w("off", 2, 3), DV, F0, w("lw", 0, 1), A.mult, A.add)
        turn(w("t64"), w("x64"))
        pick(w("p64", 0, 32), w("t64", 0, 32), w("oo", 0, 2))
        pick(w("p64", 32, 64), w("t64", 32, 64), w("oo", 0, 2), "s")
        for c, qs in ((0, "vsvvsvvv"), (32, "ssssssss")):
            buf = "rowv" if c else "row"
            for i in range(8):
                a, b = 2 * (i // 4) + i % 2, 2 * (i // 4) + i // 2 % 2
                copy(w(buf, 32 * a, 32 * a + 32, 32 * b, 32 * b + 32), w("p64", c, c + 32, 32 * a, 32 * a + 32), qs[i])
            copy(w(buf, 0, 64, 64, 128), w(buf, 0, 64, 0, 64), qs[7])
            copy(w(buf, 64, 128, 0, 64), w(buf, 64, 128, 64, 128), qs[7])
        turn(w("t2"), w("row"))
        ts(w("offr"), w("t2", 0, 128, st=16), -ROUND, None, A.add)
        for b in range(2):
            scatter(w("map"), w("offr", 4 * b, 4 * b + 4), w("rowv", 64 * b, 64 * b + 64))

    def newest(fillers):
        def filler(n=1):
            for _ in range(n):
                if fillers:
                    fillers.pop(0)()

        def same(c):
            s = 144 * c if c < 4 else 512 + 80 * (c - 4)
            ts(w("ee", s, s + 128 - 16 * c), w("brow", 16 * c, 128), w("tt", 16 * c, 16 * c + 1), None, A.is_equal)
        def mean(b):
            s = slice(128 * b, 128 * b + 128)
            tt(w("win%d" % b, 256, 512, st=2), w("fg", s.start, s.stop), w("dq", s.start, s.stop), A.add)
        pick(w("brow"), w("it"), w("offm"), "s")
        for b in range(4):
            pick(w("fg", 128 * b, 128 * b + 128), w("win%d" % b, 0, 256), w("offm"), "s", 0.5)
        a8 = w("tt", 0, 128, st=16)
        ts(w("fi"), a8, -7.5, 0.0625, A.add, A.mult)
        filler(2)
        ts(w("p1"), w("fi"), 16.0, H16, A.mult, A.add)
        filler(2)
        for c in range(4):
            same(c)
        tt(w("p2"), w("p1"), a8, A.add)
        for c in range(4, 8):
            same(c)
        filler()
        scan(w("sc"), w("ee"), w("kk"))
        mean(0)
        tt(w("offi", 0, 4), w("p2", 0, 4), w("sc", 127, 512, st=128), A.max)
        tt(w("offi", 4, 8), w("p2", 4, 8), w("sc", 575, 768, st=64), A.max)
        mean(1)
        scatter(w("inv"), w("offi"), w("sl"))
        mean(2)
        turn(w("t512"), w("inv", 0, 512))
        mean(3)
        tt(w("noff"), w("t512", 0, 512, st=32), w("t512", 16, 512, st=32), A.max)
        filler()

    def renew(r, fillers):
        for b in range(4):
            pick(w("nx", b, 1024, st=4), w("win%d" % b), w("noff"), "svsv"[b], 2.0)
        if fillers:
            fillers.pop(0)()
        quant("qx%d" % (r + 1), "nx", 0, 256)

    pieces = []
    for r in range(3):
        donor, asker = (rank + STEP[r]) % N, (rank - STEP[r]) % N
        c0 = 128 * r
        for b in range(4):
            if r:
                unpacked(b, "svsv"[b])
        for b in range(4):
            pick(w("mt", b, 512, st=4), w("win%d" % b, 0, 256), w("offm"), "svsv"[b], 2.0)
        if r:
            pieces.pop(0)()
        quant("qm", "mt", c0)
        if r < 2:
            for nm in ("", "_s"):
                send(donor, w("qm" + nm, c0, c0 + 128), w("qml" + nm, c0, c0 + 128), "am%d" % r)
            expect(asker, [w("qml", c0, c0 + 128), w("qml_s", c0, c0 + 128)], "am%d" % r)
            if r == 0:
                for b in range(4):
                    lists("rte", 0, b, "ssss")
                pieces = requests()
                late_constants()
                pick(w("map", 128, 256), w("it"), w("offa", 8, 16), "s")
                candidates()
                mask1()
            while r and pieces:
                pieces.pop(0)()
            layer("qml", c0, "qh", c0, "qw")
            for nm in ("", "_s"):
                send(asker, w("qh" + nm, c0, c0 + 128), w("qx%d" % r + nm, 256, 384), "ah%d" % r)
            expect(donor, [w("qx%d" % r, 256, 384), w("qx%d_s" % r, 256, 384)], "ah%d" % r)
            if r == 0:
                iota(w("ee"), [[0, 768]], 0, 0)
            while pieces:
                pieces.pop(0)()
            if r == 0:
                mask2()
        else:
            while len(pieces) > 1:
                pieces.pop(0)()
            layer("qm", c0, "qx2", 256, "qwl")
            pieces.pop(0)()
        copy(w("inv", 0, 512), w("cini"), "s")
        mm("pb0", 128, "qx%d" % r, 256, "qup")
        for b in range(4):
            mm("pa%d" % b, 128, "qe", 128 * b, "qx%d" % r, 256)
        for b in range(4):
            halve(w("dq", 128 * b, 128 * b + 128), w("pa%d" % b, 0, 128))
        if r == 0:
            for b in range(4):
                copy(w("win%d" % b, 256, 512), w("ee", 0, 256), "s")
        repair()
        if r == 2:
            dma("y", T.fo[:], T.map[0:1, 0:2048], [w("map", 0, 2048)], ())
        hops(places=r < 2)
        pieces = requests() if r < 2 else []
        newest(pieces)
        renew(r, pieces)
        if r < 2:
            unpack(r + 1)
            for _ in range(2):
                pieces.pop(0)()
    dma("y", T.oc[:], T.qx3[:, 0:256].bitcast(dt.uint8), [w("qx3", 0, 256)], ())
    for k in range(4):
        dma("s", T.osc[4 * k:4 * k + 4, :], T.qx3_s[32 * k:32 * k + 4, 0:256], [w("qx3_s", 0, 256)], ())
    for b in range(2):
        c = 128 * b
        mm("pb%d" % (1 + b), 128, "qv", 0, "qx3", c)
        copy(w("yt", c, c + 128), w("pb%d" % (1 + b), 0, 128), "vs"[b])
        dma("ys"[b], T.y[:, c:c + 128], T.yt[:, c:c + 128], [w("yt", c, c + 128)], ())
    for sem, n in count.items():
        if known["g"].get(sem, 0) < n:
            g.wait_ge(T.sem[sem], n)
